import numpy as np
import ml_dtypes


def mxq(x, axis, fmt="e4m3"):
    dtype, down = {"e4m3": (ml_dtypes.float8_e4m3fn, 7), "e5m2": (ml_dtypes.float8_e5m2, 14)}[fmt]
    v = np.moveaxis(np.asarray(x, np.float32).astype(ml_dtypes.bfloat16).astype(np.float64), axis, -1)
    blocks = v.reshape(v.shape[:-1] + (-1, 32))
    amax = np.abs(blocks).max(-1, keepdims=True)
    byte = np.maximum(np.where(amax > 0, np.frexp(amax)[1] - 1 + 127, 0) - down, 1)
    scale = np.exp2(byte - 127.0)
    codes = (blocks / scale).astype(np.float32).astype(dtype).astype(np.float64)
    return np.moveaxis((codes * scale).reshape(v.shape), -1, axis)


WIDE = False


def mx_kscale(k):
    if not WIDE:
        return np.ones(k)
    levels = np.array([10, -10, 5, -5, 0])
    if k % 512:
        return np.exp2(np.random.permutation(np.resize(levels, k // 32))).repeat(32)
    a = np.empty((k // 512, 16))
    for p in range(k // 512):
        a[p, :8] = np.random.permutation(np.resize(levels, 8))
        for g in range(8):
            far = levels[np.abs(levels - a[p, g]) >= 10]
            a[p, g + 8] = far[np.random.randint(len(far))]
    return np.exp2(a.ravel()).repeat(32)


def f64(x):
    return np.asarray(x).astype(np.float64)


def striped(idx):
    return np.tile(idx.reshape(-1, 16).T, (8, 1)).astype(np.uint16)


def unstriped(offs):
    return offs[:16].T.reshape(-1).astype(np.int64)


def pack_weight(w):
    k, n = w.shape
    w = f64(np.asarray(w, np.float32).astype(ml_dtypes.bfloat16)).reshape(k // 32, 32, n)
    amax = np.abs(w).max(1)
    byte = np.clip(np.where(amax > 0, np.frexp(amax)[1] - 1 + 127 - 7, 1), 1, 254)
    scaled = (w * np.exp2(127.0 - byte)[:, None, :]).reshape(k, n).astype(np.float32)
    words = np.ascontiguousarray(scaled.reshape(k // 512, 128, 4, n).transpose(0, 1, 3, 2)).astype(ml_dtypes.float8_e4m3fn).view(np.uint8)
    return words, np.ascontiguousarray(byte.astype(np.uint8).reshape(k // 512, 16, n))


def unpack_weight(words, scales):
    g, p, n, _ = words.shape
    vals = np.ascontiguousarray(words).view(ml_dtypes.float8_e4m3fn).astype(np.float64) * np.repeat(np.exp2(scales.astype(np.float64) - 127.0), 8, axis=1)[..., None]
    return vals.transpose(0, 1, 3, 2).reshape(g * 512, n)


def sigmoid(v):
    return 1.0 / (1.0 + np.exp(-np.maximum(v, -700.0)))


K, T, S, V, N = 512, 4096, 1536, 384, 256


def setup_inputs():
    n = np.random.standard_normal
    s = mx_kscale(K)[:, None]
    packed_w1 = pack_weight(n((K, N)) / np.sqrt(K) / s)
    return {
        "xT": (n((K, T)) * s).astype(np.float32),
        "w1_words": packed_w1[0],
        "w1_scales": packed_w1[1],
        "offs": striped(np.random.permutation(T)[:S]),
    }


def reference(xT, w1_words, w1_scales, offs):
    xq = mxq(f64(xT)[:, unstriped(offs)], 0, "e4m3")
    y = sigmoid(unpack_weight(w1_words, w1_scales).T @ xq)
    return ((y[:, :V] * y[:, V:2 * V]) * y[:, 2 * V:3 * V]) * y[:, 3 * V:4 * V]

@@ -1,0 +1,105 @@
+from contextlib import ExitStack
+
+import concourse.mybir as mybir
+
+K, T, S, V, N, D = 512, 4096, 1536, 384, 256, 4
+FLOPS = 2 * K * N * S
+
+F32 = mybir.dt.float32
+BF16 = mybir.dt.bfloat16
+I32 = mybir.dt.int32
+U32 = mybir.dt.uint32
+U16 = mybir.dt.uint16
+U8 = mybir.dt.uint8
+FP8X4 = mybir.dt.float8_e4m3fn_x4
+COPY = mybir.ActivationFunctionType.Copy
+SIGMOID = mybir.ActivationFunctionType.Sigmoid
+MULT = mybir.AluOpType.mult
+
+P = 128
+PACK = 4
+GATHER = 512
+UNIT = 128
+LOAD_WIDTHS = [[4096], [4096], [2048, 2048], [2048, 1024, 512, 512]]
+BANK_UNITS = [((0, 0), (1, 0)), ((0, 1), (1, 1)), ((2, 0), (2, 1)), ((0, 2), (1, 2)), ((2, 2), (3, 0)), ((3, 1), (3, 2))]
+
+
+def tile_picked_andpool_none_e_kernel(tc, xT, w1_words, w1_scales, offs, out):
+    nc = tc.nc
+    with ExitStack() as ctx:
+        keep = ctx.enter_context(tc.tile_pool(name="keep", bufs=1))
+        psum = ctx.enter_context(tc.psum_pool(name="psum", bufs=1))
+
+        offsets = keep.tile([P, S // 16], U16, name="offsets")
+        w_codes = keep.tile([P, N], U32, name="w_codes", align_bytes=64)
+        w_scales = keep.tile([P, N], U8, name="w_scales", align_bytes=64)
+        nc.vector.memset(w_scales[:].bitcast(I32), 0)
+        warm = keep.tile([P, 1], F32, name="warm")
+        warm_out = keep.tile([P, 1], F32, name="warm_out")
+        nc.vector.memset(warm[:], 0.0)
+        nc.scalar.activation(warm_out[:], warm[:], SIGMOID)
+
+        planes = xT.rearrange("(p j) t -> p j t", j=PACK)
+        x32 = [keep.tile([P, T], F32, name=f"x32_{j}") for j in range(PACK)]
+        x16 = [keep.tile([P, T], BF16, name=f"x16_{j}") for j in range(PACK)]
+        picked = [keep.tile([P, GATHER, PACK], BF16, name=f"picked_{g}", align_bytes=64) for g in range(S // GATHER)]
+
+        for j in range(PACK):
+            c0 = 0
+            for width in LOAD_WIDTHS[j]:
+                nc.sync.dma_start(out=x32[j][:, c0 : c0 + width], in_=planes[:, j, c0 : c0 + width])
+                if j == 0 and c0 == 0:
+                    nc.sync.dma_start(offsets[:], offs)
+                nc.vector.tensor_copy(out=x16[j][:, c0 : c0 + width], in_=x32[j][:, c0 : c0 + width])
+                c0 = c0 + width
+            for g in range(S // GATHER):
+                entries = offsets[:, g * GATHER // 16 : (g + 1) * GATHER // 16]
+                if g in (0,):
+                    nc.vector.tensor_copy(out=picked[g][:, :, j], in_=x32[j][:].indirect(entries))
+                else:
+                    nc.scalar.activation(picked[g][:, :, j], x16[j][:].indirect(entries), COPY)
+
+        nc.sync.dma_start(out=w_codes[:].bitcast(I32), in_=w1_words[0].rearrange("p n t -> p (n t)").bitcast(I32))
+        for q in range(4):
+            nc.sync.dma_start(out=w_scales[32 * q : 32 * q + 4, :].bitcast(I32), in_=w1_scales[0, 4 * q : 4 * q + 4, :].bitcast(I32))
+
+        x_codes = [keep.tile([P, GATHER], U32, name=f"x_codes_{g}", align_bytes=64) for g in range(S // GATHER)]
+        x_scales = [keep.tile([P, GATHER], U8, name=f"x_scales_{g}", align_bytes=64) for g in range(S // GATHER)]
+        for g in range(S // GATHER):
+            nc.vector.quantize_mx(out=x_codes[g][:].bitcast(FP8X4), scales=x_scales[g][:], in_=picked[g][:].rearrange("p n j -> p (n j)"))
+
+        truth = {}
+        for b, units in enumerate(BANK_UNITS):
+            bank = psum.tile([P, 2, 2, UNIT], F32, name=f"bank_{b}")
+            y = keep.tile([P, 2, 2, UNIT], F32, name=f"y_{b}")
+            for i, (d, r) in enumerate(units):
+                g, first = divmod(d * V + r * UNIT, GATHER)
+                for h in range(2):
+                    nc.tensor.matmul_mx(
+                        out=bank[:, i, h, :],
+                        lhsT=w_codes[:, h * P : (h + 1) * P].bitcast(FP8X4),
+                        lhsT_scale=w_scales[:, h * P : (h + 1) * P],
+                        rhs=x_codes[g][:, first : first + UNIT].bitcast(FP8X4),
+                        rhs_scale=x_scales[g][:, first : first + UNIT],
+                        start=True,
+                        stop=True,
+                    )
+                truth[(d, r)] = y[:, i, :, :]
+            if b < len(BANK_UNITS) - 2:
+                nc.scalar.activation(y[:].rearrange("p i h n -> p (i h n)"), bank[:].rearrange("p i h n -> p (i h n)"), SIGMOID)
+            else:
+                for i in range(2):
+                    nc.scalar.activation(y[:, i, :, :].rearrange("p h n -> p (h n)"), bank[:, i, :, :].rearrange("p h n -> p (h n)"), SIGMOID)
+
+        out_view = out.rearrange("(h p) v -> p h v", p=P)
+        running = {}
+        for b, units in enumerate(BANK_UNITS):
+            for d, r in units:
+                if d == 0:
+                    running[r] = truth[(d, r)]
+                else:
+                    product = keep.tile([P, 2, UNIT], F32, name=f"product_{d}_{r}")
+                    nc.vector.tensor_tensor(product[:], running[r], truth[(d, r)], MULT)
+                    running[r] = product[:]
+                    if d == D - 1:
+                        nc.sync.dma_start(out=out_view[:, :, r * UNIT : (r + 1) * UNIT], in_=product[:])

@@ -18,10 +18,10 @@ MULT = mybir.AluOpType.mult
 
 P = 128
 PACK = 4
-GATHER = 512
-UNIT = 128
-LOAD_WIDTHS = [[4096], [4096], [2048, 2048], [2048, 1024, 512, 512]]
-BANK_UNITS = [((0, 0), (1, 0)), ((0, 1), (1, 1)), ((2, 0), (2, 1)), ((0, 2), (1, 2)), ((2, 2), (3, 0)), ((3, 1), (3, 2))]
+RULES = 128
+RANGES = V // RULES
+HALF = S // 2
+LOADS = [[(2048, True), (1536, True), (512, False)]] * 3 + [[(2048, True), (1024, True), (512, False), (512, False)]]
 
 
 def tile_picked_andpool_none_e_kernel(tc, xT, w1_words, w1_scales, offs, out):
@@ -42,64 +42,61 @@ def tile_picked_andpool_none_e_kernel(tc, xT, w1_words, w1_scales, offs, out):
         planes = xT.rearrange("(p j) t -> p j t", j=PACK)
         x32 = [keep.tile([P, T], F32, name=f"x32_{j}") for j in range(PACK)]
         x16 = [keep.tile([P, T], BF16, name=f"x16_{j}") for j in range(PACK)]
-        picked = [keep.tile([P, GATHER, PACK], BF16, name=f"picked_{g}", align_bytes=64) for g in range(S // GATHER)]
+        picked = [keep.tile([P, RANGES, 2, RULES, PACK], BF16, name=f"picked_{g}", align_bytes=64) for g in range(2)]
 
         for j in range(PACK):
             c0 = 0
-            for width in LOAD_WIDTHS[j]:
-                nc.sync.dma_start(out=x32[j][:, c0 : c0 + width], in_=planes[:, j, c0 : c0 + width])
+            for width, on_vector in LOADS[j]:
+                cols = slice(c0, c0 + width)
+                nc.sync.dma_start(out=x32[j][:, cols], in_=planes[:, j, cols])
                 if j == 0 and c0 == 0:
                     nc.sync.dma_start(offsets[:], offs)
-                nc.vector.tensor_copy(out=x16[j][:, c0 : c0 + width], in_=x32[j][:, c0 : c0 + width])
-                c0 = c0 + width
-            for g in range(S // GATHER):
-                entries = offsets[:, g * GATHER // 16 : (g + 1) * GATHER // 16]
-                if g in (0,):
-                    nc.vector.tensor_copy(out=picked[g][:, :, j], in_=x32[j][:].indirect(entries))
+                if on_vector:
+                    nc.vector.tensor_copy(out=x16[j][:, cols], in_=x32[j][:, cols])
                 else:
-                    nc.scalar.activation(picked[g][:, :, j], x16[j][:].indirect(entries), COPY)
+                    nc.scalar.copy(out=x16[j][:, cols], in_=x32[j][:, cols])
+                c0 = c0 + width
+            into = [picked[g][:, :, :, :, j].rearrange("p r e n -> p e r n") for g in range(2)]
+            nc.vector.tensor_copy(out=into[0], in_=x32[j][:].indirect(offsets[:, 0 : HALF // 16]))
+            nc.scalar.activation(into[1], x16[j][:].indirect(offsets[:, HALF // 16 : S // 16]), COPY)
 
         nc.sync.dma_start(out=w_codes[:].bitcast(I32), in_=w1_words[0].rearrange("p n t -> p (n t)").bitcast(I32))
         for q in range(4):
             nc.sync.dma_start(out=w_scales[32 * q : 32 * q + 4, :].bitcast(I32), in_=w1_scales[0, 4 * q : 4 * q + 4, :].bitcast(I32))
 
-        x_codes = [keep.tile([P, GATHER], U32, name=f"x_codes_{g}", align_bytes=64) for g in range(S // GATHER)]
-        x_scales = [keep.tile([P, GATHER], U8, name=f"x_scales_{g}", align_bytes=64) for g in range(S // GATHER)]
-        for g in range(S // GATHER):
-            nc.vector.quantize_mx(out=x_codes[g][:].bitcast(FP8X4), scales=x_scales[g][:], in_=picked[g][:].rearrange("p n j -> p (n j)"))
-
-        truth = {}
-        for b, units in enumerate(BANK_UNITS):
-            bank = psum.tile([P, 2, 2, UNIT], F32, name=f"bank_{b}")
-            y = keep.tile([P, 2, 2, UNIT], F32, name=f"y_{b}")
-            for i, (d, r) in enumerate(units):
-                g, first = divmod(d * V + r * UNIT, GATHER)
+        banks = {}
+        for g in range(2):
+            for r in range(RANGES):
+                x_codes = keep.tile([P, 2 * RULES], U32, name=f"x_codes_{g}_{r}", align_bytes=64)
+                x_scales = keep.tile([P, 2 * RULES], U8, name=f"x_scales_{g}_{r}", align_bytes=64)
+                nc.vector.quantize_mx(out=x_codes[:].bitcast(FP8X4), scales=x_scales[:], in_=picked[g][:, r].rearrange("p e n j -> p (e n j)"))
+                bank = psum.tile([P, 2, 2, RULES], F32, name=f"bank_{g}_{r}")
                 for h in range(2):
                     nc.tensor.matmul_mx(
-                        out=bank[:, i, h, :],
+                        out=bank[:, h].rearrange("p e n -> p (e n)"),
                         lhsT=w_codes[:, h * P : (h + 1) * P].bitcast(FP8X4),
                         lhsT_scale=w_scales[:, h * P : (h + 1) * P],
-                        rhs=x_codes[g][:, first : first + UNIT].bitcast(FP8X4),
-                        rhs_scale=x_scales[g][:, first : first + UNIT],
+                        rhs=x_codes[:].bitcast(FP8X4),
+                        rhs_scale=x_scales[:],
                         start=True,
                         stop=True,
                     )
-                truth[(d, r)] = y[:, i, :, :]
-            if b < len(BANK_UNITS) - 2:
-                nc.scalar.activation(y[:].rearrange("p i h n -> p (i h n)"), bank[:].rearrange("p i h n -> p (i h n)"), SIGMOID)
-            else:
-                for i in range(2):
-                    nc.scalar.activation(y[:, i, :, :].rearrange("p h n -> p (h n)"), bank[:, i, :, :].rearrange("p h n -> p (h n)"), SIGMOID)
+                banks[(g, r)] = bank
 
         out_view = out.rearrange("(h p) v -> p h v", p=P)
-        running = {}
-        for b, units in enumerate(BANK_UNITS):
-            for d, r in units:
-                if d == 0:
-                    running[r] = truth[(d, r)]
-                else:
-                    product = keep.tile([P, 2, UNIT], F32, name=f"product_{d}_{r}")
-                    nc.vector.tensor_tensor(product[:], running[r], truth[(d, r)], MULT)
-                    running[r] = product[:]
-                    if d == D - 1:
-                        nc.sync.dma_start(out=out_view[:, :, r * UNIT : (r + 1) * UNIT], in_=product[:])
+        first_two = []
+        for r in range(RANGES):
+            y = keep.tile([P, 2, 2, RULES], F32, name=f"y01_{r}")
+            nc.scalar.activation(y[:].rearrange("p h e n -> p (h e n)"), banks[(0, r)][:].rearrange("p h e n -> p (h e n)"), SIGMOID)
+            product = keep.tile([P, 2, RULES], F32, name=f"product01_{r}")
+            nc.vector.tensor_tensor(product[:], y[:, :, 0, :], y[:, :, 1, :], MULT)
+            first_two.append(product)
+        running = first_two
+        for e, r in [(0, 0), (0, 1), (1, 0), (0, 2), (1, 1), (1, 2)]:
+            y = keep.tile([P, 2, RULES], F32, name=f"y_{e}_{r}")
+            nc.scalar.activation(y[:], banks[(1, r)][:, :, e, :], SIGMOID)
+            product = keep.tile([P, 2, RULES], F32, name=f"product_{e}_{r}")
+            nc.vector.tensor_tensor(product[:], running[r][:], y[:], MULT)
+            running = running[:r] + [product] + running[r + 1 :]
+            if e == 1:
+                nc.sync.dma_start(out=out_view[:, :, r * RULES : (r + 1) * RULES], in_=product[:])

@@ -21,7 +21,8 @@ PACK = 4
 RULES = 128
 RANGES = V // RULES
 HALF = S // 2
-LOADS = [[(2048, True), (1536, True), (512, False)]] * 3 + [[(2048, True), (1024, True), (512, False), (512, False)]]
+LOADS = [[(3072, 2048), (1024, 704)], [(2560, 1920), (1536, 1024)], [(2560, 1920), (1536, 1024)], [(2560, 1920), (1024, 704), (384, 256), (128, 0)]]
+QUANTISE = [[(0, 128), (128, 256), (256, 768)], [(0, 256), (256, 768)]]
 
 
 def tile_picked_andpool_none_e_kernel(tc, xT, w1_words, w1_scales, offs, out):
@@ -47,15 +48,15 @@ def tile_picked_andpool_none_e_kernel(tc, xT, w1_words, w1_scales, offs, out):
         for j in range(PACK):
             c0 = 0
             for width, on_vector in LOADS[j]:
-                cols = slice(c0, c0 + width)
-                nc.sync.dma_start(out=x32[j][:, cols], in_=planes[:, j, cols])
+                mid, c1 = c0 + on_vector, c0 + width
+                nc.sync.dma_start(out=x32[j][:, c0:c1], in_=planes[:, j, c0:c1])
                 if j == 0 and c0 == 0:
                     nc.sync.dma_start(offsets[:], offs)
-                if on_vector:
-                    nc.vector.tensor_copy(out=x16[j][:, cols], in_=x32[j][:, cols])
-                else:
-                    nc.scalar.copy(out=x16[j][:, cols], in_=x32[j][:, cols])
-                c0 = c0 + width
+                if mid > c0:
+                    nc.vector.tensor_copy(out=x16[j][:, c0:mid], in_=x32[j][:, c0:mid])
+                if mid < c1:
+                    nc.scalar.copy(out=x16[j][:, mid:c1], in_=x32[j][:, mid:c1])
+                c0 = c1
             into = [picked[g][:, :, :, :, j].rearrange("p r e n -> p e r n") for g in range(2)]
             nc.vector.tensor_copy(out=into[0], in_=x32[j][:].indirect(offsets[:, 0 : HALF // 16]))
             nc.scalar.activation(into[1], x16[j][:].indirect(offsets[:, HALF // 16 : S // 16]), COPY)
@@ -64,39 +65,51 @@ def tile_picked_andpool_none_e_kernel(tc, xT, w1_words, w1_scales, offs, out):
         for q in range(4):
             nc.sync.dma_start(out=w_scales[32 * q : 32 * q + 4, :].bitcast(I32), in_=w1_scales[0, 4 * q : 4 * q + 4, :].bitcast(I32))
 
-        banks = {}
+        def sigmoid_of_product(into, codes, scales, halves):
+            width = codes.shape[1]
+            bank = psum.tile([P, len(halves), width], F32, name="bank", bufs=8)
+            for place, h in enumerate(halves):
+                nc.tensor.matmul_mx(
+                    out=bank[:, place],
+                    lhsT=w_codes[:, h * P : (h + 1) * P].bitcast(FP8X4),
+                    lhsT_scale=w_scales[:, h * P : (h + 1) * P],
+                    rhs=codes.bitcast(FP8X4),
+                    rhs_scale=scales,
+                    start=True,
+                    stop=True,
+                )
+            nc.scalar.activation(into, bank[:], SIGMOID)
+
+        x_codes = [keep.tile([P, HALF], U32, name=f"x_codes_{g}", align_bytes=64) for g in range(2)]
+        x_scales = [keep.tile([P, HALF], U8, name=f"x_scales_{g}", align_bytes=64) for g in range(2)]
         for g in range(2):
-            for r in range(RANGES):
-                x_codes = keep.tile([P, 2 * RULES], U32, name=f"x_codes_{g}_{r}", align_bytes=64)
-                x_scales = keep.tile([P, 2 * RULES], U8, name=f"x_scales_{g}_{r}", align_bytes=64)
-                nc.vector.quantize_mx(out=x_codes[:].bitcast(FP8X4), scales=x_scales[:], in_=picked[g][:, r].rearrange("p e n j -> p (e n j)"))
-                bank = psum.tile([P, 2, 2, RULES], F32, name=f"bank_{g}_{r}")
-                for h in range(2):
-                    nc.tensor.matmul_mx(
-                        out=bank[:, h].rearrange("p e n -> p (e n)"),
-                        lhsT=w_codes[:, h * P : (h + 1) * P].bitcast(FP8X4),
-                        lhsT_scale=w_scales[:, h * P : (h + 1) * P],
-                        rhs=x_codes[:].bitcast(FP8X4),
-                        rhs_scale=x_scales[:],
-                        start=True,
-                        stop=True,
-                    )
-                banks[(g, r)] = bank
+            flat = picked[g][:].rearrange("p r e n j -> p (r e n j)")
+            for c0, c1 in QUANTISE[g]:
+                nc.vector.quantize_mx(out=x_codes[g][:, c0:c1].bitcast(FP8X4), scales=x_scales[g][:, c0:c1], in_=flat[:, PACK * c0 : PACK * c1])
 
         out_view = out.rearrange("(h p) v -> p h v", p=P)
-        first_two = []
+        running = []
         for r in range(RANGES):
             y = keep.tile([P, 2, 2, RULES], F32, name=f"y01_{r}")
-            nc.scalar.activation(y[:].rearrange("p h e n -> p (h e n)"), banks[(0, r)][:].rearrange("p h e n -> p (h e n)"), SIGMOID)
+            for i in range(2):
+                if r < 1:
+                    cols = slice((2 * r + i) * RULES, (2 * r + i + 1) * RULES)
+                    sigmoid_of_product(y[:, :, i, :], x_codes[0][:, cols], x_scales[0][:, cols], [0, 1])
+                else:
+                    cols = slice(2 * r * RULES, 2 * (r + 1) * RULES)
+                    sigmoid_of_product(y[:, i : i + 1].rearrange("p h e n -> p h (e n)"), x_codes[0][:, cols], x_scales[0][:, cols], [i])
             product = keep.tile([P, 2, RULES], F32, name=f"product01_{r}")
             nc.vector.tensor_tensor(product[:], y[:, :, 0, :], y[:, :, 1, :], MULT)
-            first_two.append(product)
-        running = first_two
+            running.append(product)
         for e, r in [(0, 0), (0, 1), (1, 0), (0, 2), (1, 1), (1, 2)]:
-            y = keep.tile([P, 2, RULES], F32, name=f"y_{e}_{r}")
-            nc.scalar.activation(y[:], banks[(1, r)][:, :, e, :], SIGMOID)
-            product = keep.tile([P, 2, RULES], F32, name=f"product_{e}_{r}")
-            nc.vector.tensor_tensor(product[:], running[r][:], y[:], MULT)
+            cols = slice((2 * r + e) * RULES, (2 * r + e + 1) * RULES)
+            last = (e, r) == (1, 2)
+            for halves in ([[0], [1]] if last else [[0, 1]]):
+                hs = slice(halves[0], halves[-1] + 1)
+                y = keep.tile([P, len(halves), RULES], F32, name=f"y_{e}_{r}_{halves[0]}")
+                sigmoid_of_product(y[:], x_codes[1][:, cols], x_scales[1][:, cols], halves)
+                product = keep.tile([P, len(halves), RULES], F32, name=f"product_{e}_{r}_{halves[0]}")
+                nc.vector.tensor_tensor(product[:], running[r][:, hs], y[:], MULT)
+                if e == 1:
+                    nc.sync.dma_start(out=out_view[:, hs, r * RULES : (r + 1) * RULES], in_=product[:])
             running = running[:r] + [product] + running[r + 1 :]
-            if e == 1:
-                nc.sync.dma_start(out=out_view[:, :, r * RULES : (r + 1) * RULES], in_=product[:])

@@ -20,9 +20,9 @@ P = 128
 PACK = 4
 RULES = 128
 RANGES = V // RULES
-HALF = S // 2
-LOADS = [[(3072, 2048), (1024, 704)], [(2560, 1920), (1536, 1024)], [(2560, 1920), (1536, 1024)], [(2560, 1920), (1024, 704), (384, 256), (128, 0)]]
-QUANTISE = [[(0, 128), (128, 256), (256, 768)], [(0, 256), (256, 768)]]
+ON_VECTOR = 704
+LOADS = [[(3072, 2304), (1024, 704)], [(2560, 2176), (1536, 1024)], [(2560, 2176), (1536, 1024)], [(2560, 2176), (1024, 640), (512, 0)]]
+QUANTISE = [(0, 128), (128, 384), (384, 640), (640, 1152), (1152, 1408), (1408, 1536)]
 
 
 def tile_picked_andpool_none_e_kernel(tc, xT, w1_words, w1_scales, offs, out):
@@ -43,7 +43,7 @@ def tile_picked_andpool_none_e_kernel(tc, xT, w1_words, w1_scales, offs, out):
         planes = xT.rearrange("(p j) t -> p j t", j=PACK)
         x32 = [keep.tile([P, T], F32, name=f"x32_{j}") for j in range(PACK)]
         x16 = [keep.tile([P, T], BF16, name=f"x16_{j}") for j in range(PACK)]
-        picked = [keep.tile([P, RANGES, 2, RULES, PACK], BF16, name=f"picked_{g}", align_bytes=64) for g in range(2)]
+        picked = keep.tile([P, S, PACK], BF16, name="picked", align_bytes=64)
 
         for j in range(PACK):
             c0 = 0
@@ -54,12 +54,14 @@ def tile_picked_andpool_none_e_kernel(tc, xT, w1_words, w1_scales, offs, out):
                     nc.sync.dma_start(offsets[:], offs)
                 if mid > c0:
                     nc.vector.tensor_copy(out=x16[j][:, c0:mid], in_=x32[j][:, c0:mid])
+                if mid == c0:
+                    mid = (c0 + c1) // 2
+                    nc.gpsimd.tensor_copy(out=x16[j][:, c0:mid], in_=x32[j][:, c0:mid])
                 if mid < c1:
                     nc.scalar.copy(out=x16[j][:, mid:c1], in_=x32[j][:, mid:c1])
                 c0 = c1
-            into = [picked[g][:, :, :, :, j].rearrange("p r e n -> p e r n") for g in range(2)]
-            nc.vector.tensor_copy(out=into[0], in_=x32[j][:].indirect(offsets[:, 0 : HALF // 16]))
-            nc.scalar.activation(into[1], x16[j][:].indirect(offsets[:, HALF // 16 : S // 16]), COPY)
+            nc.vector.tensor_copy(out=picked[:, :ON_VECTOR, j], in_=x32[j][:].indirect(offsets[:, : ON_VECTOR // 16]))
+            nc.scalar.activation(picked[:, ON_VECTOR:, j], x16[j][:].indirect(offsets[:, ON_VECTOR // 16 :]), COPY)
 
         nc.sync.dma_start(out=w_codes[:].bitcast(I32), in_=w1_words[0].rearrange("p n t -> p (n t)").bitcast(I32))
         for q in range(4):
@@ -80,36 +82,25 @@ def tile_picked_andpool_none_e_kernel(tc, xT, w1_words, w1_scales, offs, out):
                 )
             nc.scalar.activation(into, bank[:], SIGMOID)
 
-        x_codes = [keep.tile([P, HALF], U32, name=f"x_codes_{g}", align_bytes=64) for g in range(2)]
-        x_scales = [keep.tile([P, HALF], U8, name=f"x_scales_{g}", align_bytes=64) for g in range(2)]
-        for g in range(2):
-            flat = picked[g][:].rearrange("p r e n j -> p (r e n j)")
-            for c0, c1 in QUANTISE[g]:
-                nc.vector.quantize_mx(out=x_codes[g][:, c0:c1].bitcast(FP8X4), scales=x_scales[g][:, c0:c1], in_=flat[:, PACK * c0 : PACK * c1])
+        x_codes = keep.tile([P, S], U32, name="x_codes", align_bytes=64)
+        x_scales = keep.tile([P, S], U8, name="x_scales", align_bytes=64)
+        for e0, e1 in QUANTISE:
+            nc.vector.quantize_mx(out=x_codes[:, e0:e1].bitcast(FP8X4), scales=x_scales[:, e0:e1], in_=picked[:, e0:e1].rearrange("p n j -> p (n j)"))
 
         out_view = out.rearrange("(h p) v -> p h v", p=P)
-        running = []
-        for r in range(RANGES):
-            y = keep.tile([P, 2, 2, RULES], F32, name=f"y01_{r}")
-            for i in range(2):
-                if r < 1:
-                    cols = slice((2 * r + i) * RULES, (2 * r + i + 1) * RULES)
-                    sigmoid_of_product(y[:, :, i, :], x_codes[0][:, cols], x_scales[0][:, cols], [0, 1])
-                else:
-                    cols = slice(2 * r * RULES, 2 * (r + 1) * RULES)
-                    sigmoid_of_product(y[:, i : i + 1].rearrange("p h e n -> p h (e n)"), x_codes[0][:, cols], x_scales[0][:, cols], [i])
-            product = keep.tile([P, 2, RULES], F32, name=f"product01_{r}")
-            nc.vector.tensor_tensor(product[:], y[:, :, 0, :], y[:, :, 1, :], MULT)
-            running.append(product)
-        for e, r in [(0, 0), (0, 1), (1, 0), (0, 2), (1, 1), (1, 2)]:
-            cols = slice((2 * r + e) * RULES, (2 * r + e + 1) * RULES)
-            last = (e, r) == (1, 2)
+        running = {}
+        for d, r in [(0, 0), (0, 1), (1, 0), (1, 1), (0, 2), (1, 2), (2, 0), (2, 1), (3, 0), (2, 2), (3, 1), (3, 2)]:
+            entries = slice(d * V + r * RULES, d * V + (r + 1) * RULES)
+            last = (d, r) == (D - 1, RANGES - 1)
             for halves in ([[0], [1]] if last else [[0, 1]]):
                 hs = slice(halves[0], halves[-1] + 1)
-                y = keep.tile([P, len(halves), RULES], F32, name=f"y_{e}_{r}_{halves[0]}")
-                sigmoid_of_product(y[:], x_codes[1][:, cols], x_scales[1][:, cols], halves)
-                product = keep.tile([P, len(halves), RULES], F32, name=f"product_{e}_{r}_{halves[0]}")
-                nc.vector.tensor_tensor(product[:], running[r][:, hs], y[:], MULT)
-                if e == 1:
+                y = keep.tile([P, len(halves), RULES], F32, name=f"y_{d}_{r}_{halves[0]}")
+                sigmoid_of_product(y[:], x_codes[:, entries], x_scales[:, entries], halves)
+                if d == 0:
+                    product = y
+                else:
+                    product = keep.tile([P, len(halves), RULES], F32, name=f"product_{d}_{r}_{halves[0]}")
+                    nc.vector.tensor_tensor(product[:], running[r][:, hs], y[:], MULT)
+                if d == D - 1:
                     nc.sync.dma_start(out=out_view[:, hs, r * RULES : (r + 1) * RULES], in_=product[:])
-            running = running[:r] + [product] + running[r + 1 :]
+            running[r] = product

@@ -18,11 +18,33 @@ MULT = mybir.AluOpType.mult
 
 P = 128
 PACK = 4
-RULES = 128
-RANGES = V // RULES
-ON_VECTOR = 704
-LOADS = [[(3072, 2304), (1024, 704)], [(2560, 2176), (1536, 1024)], [(2560, 2176), (1536, 1024)], [(2560, 2176), (1024, 640), (512, 0)]]
-QUANTISE = [(0, 128), (128, 384), (384, 640), (640, 1152), (1152, 1408), (1408, 1536)]
+UNIT = 128
+RANGES = V // UNIT
+PER_COLUMN = 16
+PSUM_BANKS = 8
+
+ON_VECTOR = S // 2
+
+PLAIN_ON_VECTOR = 2 * UNIT
+PLAIN_ON_SCALAR = UNIT
+
+FIRST_PLANE = [(3072, 2048), (1024, 704)]
+MIDDLE_PLANE = [(2560, 1920), (1536, 1024)]
+LAST_PLANE = [(2560, 1920), (1152, 704), (384, 0)]
+LOADS = [FIRST_PLANE, MIDDLE_PLANE, MIDDLE_PLANE, LAST_PLANE]
+
+QUANTISE_UNITS = [1, 1, 2, 2, 1, 4, 1]
+
+
+def unit_order():
+    order = []
+    for even in range(0, D, 2):
+        for step in range(RANGES + 1):
+            if step < RANGES:
+                order.append((even, step))
+            if step > 0:
+                order.append((even + 1, step - 1))
+    return order
 
 
 def tile_picked_andpool_none_e_kernel(tc, xT, w1_words, w1_scales, offs, out):
@@ -31,10 +53,11 @@ def tile_picked_andpool_none_e_kernel(tc, xT, w1_words, w1_scales, offs, out):
         keep = ctx.enter_context(tc.tile_pool(name="keep", bufs=1))
         psum = ctx.enter_context(tc.psum_pool(name="psum", bufs=1))
 
-        offsets = keep.tile([P, S // 16], U16, name="offsets")
+        offsets = keep.tile([P, S // PER_COLUMN], U16, name="offsets")
         w_codes = keep.tile([P, N], U32, name="w_codes", align_bytes=64)
         w_scales = keep.tile([P, N], U8, name="w_scales", align_bytes=64)
         nc.vector.memset(w_scales[:].bitcast(I32), 0)
+
         warm = keep.tile([P, 1], F32, name="warm")
         warm_out = keep.tile([P, 1], F32, name="warm_out")
         nc.vector.memset(warm[:], 0.0)
@@ -45,62 +68,82 @@ def tile_picked_andpool_none_e_kernel(tc, xT, w1_words, w1_scales, offs, out):
         x16 = [keep.tile([P, T], BF16, name=f"x16_{j}") for j in range(PACK)]
         picked = keep.tile([P, S, PACK], BF16, name="picked", align_bytes=64)
 
+        def gather_on_vector(into, j, e0, e1):
+            nc.vector.tensor_copy(out=into, in_=x32[j][:].indirect(offsets[:, e0 // PER_COLUMN : e1 // PER_COLUMN]))
+
+        def gather_on_scalar(into, j, e0, e1):
+            nc.scalar.activation(into, x16[j][:].indirect(offsets[:, e0 // PER_COLUMN : e1 // PER_COLUMN]), COPY)
+
+        def gather_plain_units(gather, j, e0, e1):
+            for first in range(e0, e1, UNIT):
+                plain = keep.tile([P, UNIT], BF16, name=f"plain_{first}")
+                gather(plain[:], j, first, first + UNIT)
+                nc.gpsimd.tensor_copy(out=picked[:, first : first + UNIT, j], in_=plain[:])
+
         for j in range(PACK):
             c0 = 0
-            for width, on_vector in LOADS[j]:
-                mid, c1 = c0 + on_vector, c0 + width
+            for width, rounded_on_vector in LOADS[j]:
+                mid, c1 = c0 + rounded_on_vector, c0 + width
                 nc.sync.dma_start(out=x32[j][:, c0:c1], in_=planes[:, j, c0:c1])
                 if j == 0 and c0 == 0:
                     nc.sync.dma_start(offsets[:], offs)
                 if mid > c0:
                     nc.vector.tensor_copy(out=x16[j][:, c0:mid], in_=x32[j][:, c0:mid])
-                if mid == c0:
-                    mid = (c0 + c1) // 2
-                    nc.gpsimd.tensor_copy(out=x16[j][:, c0:mid], in_=x32[j][:, c0:mid])
-                if mid < c1:
-                    nc.scalar.copy(out=x16[j][:, mid:c1], in_=x32[j][:, mid:c1])
+                nc.scalar.copy(out=x16[j][:, mid:c1], in_=x32[j][:, mid:c1])
                 c0 = c1
-            nc.vector.tensor_copy(out=picked[:, :ON_VECTOR, j], in_=x32[j][:].indirect(offsets[:, : ON_VECTOR // 16]))
-            nc.scalar.activation(picked[:, ON_VECTOR:, j], x16[j][:].indirect(offsets[:, ON_VECTOR // 16 :]), COPY)
+            vector_from, scalar_from = 0, ON_VECTOR
+            if j == PACK - 1:
+                vector_from, scalar_from = PLAIN_ON_VECTOR, ON_VECTOR + PLAIN_ON_SCALAR
+                gather_plain_units(gather_on_vector, j, 0, vector_from)
+                gather_plain_units(gather_on_scalar, j, ON_VECTOR, scalar_from)
+            gather_on_vector(picked[:, vector_from:ON_VECTOR, j], j, vector_from, ON_VECTOR)
+            gather_on_scalar(picked[:, scalar_from:, j], j, scalar_from, S)
 
         nc.sync.dma_start(out=w_codes[:].bitcast(I32), in_=w1_words[0].rearrange("p n t -> p (n t)").bitcast(I32))
-        for q in range(4):
+        for q in range(P // 32):
             nc.sync.dma_start(out=w_scales[32 * q : 32 * q + 4, :].bitcast(I32), in_=w1_scales[0, 4 * q : 4 * q + 4, :].bitcast(I32))
 
-        def sigmoid_of_product(into, codes, scales, halves):
-            width = codes.shape[1]
-            bank = psum.tile([P, len(halves), width], F32, name="bank", bufs=8)
+        x_codes = keep.tile([P, S], U32, name="x_codes", align_bytes=64)
+        x_scales = keep.tile([P, S], U8, name="x_scales", align_bytes=64)
+        e0 = 0
+        for units in QUANTISE_UNITS:
+            e1 = e0 + units * UNIT
+            nc.vector.quantize_mx(
+                out=x_codes[:, e0:e1].bitcast(FP8X4),
+                scales=x_scales[:, e0:e1],
+                in_=picked[:, e0:e1].rearrange("p n j -> p (n j)"),
+            )
+            e0 = e1
+
+        def truth_values(into, entries, halves):
+            bank = psum.tile([P, len(halves), UNIT], F32, name="bank", bufs=PSUM_BANKS)
             for place, h in enumerate(halves):
                 nc.tensor.matmul_mx(
                     out=bank[:, place],
                     lhsT=w_codes[:, h * P : (h + 1) * P].bitcast(FP8X4),
                     lhsT_scale=w_scales[:, h * P : (h + 1) * P],
-                    rhs=codes.bitcast(FP8X4),
-                    rhs_scale=scales,
+                    rhs=x_codes[:, entries].bitcast(FP8X4),
+                    rhs_scale=x_scales[:, entries],
                     start=True,
                     stop=True,
                 )
             nc.scalar.activation(into, bank[:], SIGMOID)
 
-        x_codes = keep.tile([P, S], U32, name="x_codes", align_bytes=64)
-        x_scales = keep.tile([P, S], U8, name="x_scales", align_bytes=64)
-        for e0, e1 in QUANTISE:
-            nc.vector.quantize_mx(out=x_codes[:, e0:e1].bitcast(FP8X4), scales=x_scales[:, e0:e1], in_=picked[:, e0:e1].rearrange("p n j -> p (n j)"))
-
         out_view = out.rearrange("(h p) v -> p h v", p=P)
-        running = {}
-        for d, r in [(0, 0), (0, 1), (1, 0), (1, 1), (0, 2), (1, 2), (2, 0), (2, 1), (3, 0), (2, 2), (3, 1), (3, 2)]:
-            entries = slice(d * V + r * RULES, d * V + (r + 1) * RULES)
-            last = (d, r) == (D - 1, RANGES - 1)
-            for halves in ([[0], [1]] if last else [[0, 1]]):
-                hs = slice(halves[0], halves[-1] + 1)
-                y = keep.tile([P, len(halves), RULES], F32, name=f"y_{d}_{r}_{halves[0]}")
-                sigmoid_of_product(y[:], x_codes[:, entries], x_scales[:, entries], halves)
+        order = unit_order()
+        so_far = {}
+        for d, r in order:
+            entries = slice(d * V + r * UNIT, d * V + (r + 1) * UNIT)
+            parts = [[0], [1]] if (d, r) == order[-1] else [[0, 1]]
+            for halves in parts:
+                rows = slice(halves[0], halves[-1] + 1)
+                truth = keep.tile([P, len(halves), UNIT], F32, name=f"truth_{d}_{r}_{halves[0]}")
+                truth_values(truth[:], entries, halves)
                 if d == 0:
-                    product = y
+                    product = truth
                 else:
-                    product = keep.tile([P, len(halves), RULES], F32, name=f"product_{d}_{r}_{halves[0]}")
-                    nc.vector.tensor_tensor(product[:], running[r][:, hs], y[:], MULT)
+                    product = keep.tile([P, len(halves), UNIT], F32, name=f"product_{d}_{r}_{halves[0]}")
+                    nc.vector.tensor_tensor(product[:], so_far[r][:, rows], truth[:], MULT)
                 if d == D - 1:
-                    nc.sync.dma_start(out=out_view[:, hs, r * RULES : (r + 1) * RULES], in_=product[:])
-            running[r] = product
+                    nc.sync.dma_start(out=out_view[:, rows, r * UNIT : (r + 1) * UNIT], in_=product[:])
+            so_far[r] = product

@@ -26,14 +26,13 @@ PSUM_BANKS = 8
 ON_VECTOR = S // 2
 
 PLAIN_ON_VECTOR = 2 * UNIT
-PLAIN_ON_SCALAR = UNIT
 
 FIRST_PLANE = [(3072, 2048), (1024, 704)]
 MIDDLE_PLANE = [(2560, 1920), (1536, 1024)]
 LAST_PLANE = [(2560, 1920), (1152, 704), (384, 0)]
 LOADS = [FIRST_PLANE, MIDDLE_PLANE, MIDDLE_PLANE, LAST_PLANE]
 
-QUANTISE_UNITS = [1, 1, 2, 2, 1, 4, 1]
+QUANTISE_UNITS = [1, 1, 2, 2, 2, 4]
 
 
 def unit_order():
@@ -91,13 +90,12 @@ def tile_picked_andpool_none_e_kernel(tc, xT, w1_words, w1_scales, offs, out):
                     nc.vector.tensor_copy(out=x16[j][:, c0:mid], in_=x32[j][:, c0:mid])
                 nc.scalar.copy(out=x16[j][:, mid:c1], in_=x32[j][:, mid:c1])
                 c0 = c1
-            vector_from, scalar_from = 0, ON_VECTOR
+            vector_from = 0
             if j == PACK - 1:
-                vector_from, scalar_from = PLAIN_ON_VECTOR, ON_VECTOR + PLAIN_ON_SCALAR
+                vector_from = PLAIN_ON_VECTOR
                 gather_plain_units(gather_on_vector, j, 0, vector_from)
-                gather_plain_units(gather_on_scalar, j, ON_VECTOR, scalar_from)
             gather_on_vector(picked[:, vector_from:ON_VECTOR, j], j, vector_from, ON_VECTOR)
-            gather_on_scalar(picked[:, scalar_from:, j], j, scalar_from, S)
+            gather_on_scalar(picked[:, ON_VECTOR:, j], j, ON_VECTOR, S)
 
         nc.sync.dma_start(out=w_codes[:].bitcast(I32), in_=w1_words[0].rearrange("p n t -> p (n t)").bitcast(I32))
         for q in range(P // 32):

@@ -25,12 +25,14 @@ PSUM_BANKS = 8
 
 ON_VECTOR = S // 2
 
-PLAIN_ON_VECTOR = 2 * UNIT
+PLAIN_PARTS = [[], [], [192], [UNIT, UNIT]]
 
-FIRST_PLANE = [(3072, 2048), (1024, 704)]
-MIDDLE_PLANE = [(2560, 1920), (1536, 1024)]
-LAST_PLANE = [(2560, 1920), (1152, 704), (384, 0)]
-LOADS = [FIRST_PLANE, MIDDLE_PLANE, MIDDLE_PLANE, LAST_PLANE]
+LOADS = [
+    [(2048, 1024), (704, 320)],
+    [(2048, 896), (768, 384)],
+    [(2048, 896), (768, 384)],
+    [(2048, 512), (768, 384), (0, 384)],
+]
 
 QUANTISE_UNITS = [1, 1, 2, 2, 2, 4]
 
@@ -73,28 +75,24 @@ def tile_picked_andpool_none_e_kernel(tc, xT, w1_words, w1_scales, offs, out):
         def gather_on_scalar(into, j, e0, e1):
             nc.scalar.activation(into, x16[j][:].indirect(offsets[:, e0 // PER_COLUMN : e1 // PER_COLUMN]), COPY)
 
-        def gather_plain_units(gather, j, e0, e1):
-            for first in range(e0, e1, UNIT):
-                plain = keep.tile([P, UNIT], BF16, name=f"plain_{first}")
-                gather(plain[:], j, first, first + UNIT)
-                nc.gpsimd.tensor_copy(out=picked[:, first : first + UNIT, j], in_=plain[:])
-
         for j in range(PACK):
             c0 = 0
-            for width, rounded_on_vector in LOADS[j]:
-                mid, c1 = c0 + rounded_on_vector, c0 + width
+            for shares in LOADS[j]:
+                c1 = c0 + sum(shares)
                 nc.sync.dma_start(out=x32[j][:, c0:c1], in_=planes[:, j, c0:c1])
                 if j == 0 and c0 == 0:
                     nc.sync.dma_start(offsets[:], offs)
-                if mid > c0:
-                    nc.vector.tensor_copy(out=x16[j][:, c0:mid], in_=x32[j][:, c0:mid])
-                nc.scalar.copy(out=x16[j][:, mid:c1], in_=x32[j][:, mid:c1])
-                c0 = c1
-            vector_from = 0
-            if j == PACK - 1:
-                vector_from = PLAIN_ON_VECTOR
-                gather_plain_units(gather_on_vector, j, 0, vector_from)
-            gather_on_vector(picked[:, vector_from:ON_VECTOR, j], j, vector_from, ON_VECTOR)
+                for round_on, width in zip((nc.vector.tensor_copy, nc.scalar.copy), shares):
+                    if width > 0:
+                        round_on(out=x16[j][:, c0 : c0 + width], in_=x32[j][:, c0 : c0 + width])
+                    c0 = c0 + width
+            e0 = 0
+            for part in PLAIN_PARTS[j]:
+                plain = keep.tile([P, part], BF16, name=f"plain_{j}_{e0}")
+                gather_on_vector(plain[:], j, e0, e0 + part)
+                nc.gpsimd.tensor_copy(out=picked[:, e0 : e0 + part, j], in_=plain[:])
+                e0 = e0 + part
+            gather_on_vector(picked[:, e0:ON_VECTOR, j], j, e0, ON_VECTOR)
             gather_on_scalar(picked[:, ON_VECTOR:, j], j, ON_VECTOR, S)
 
         nc.sync.dma_start(out=w_codes[:].bitcast(I32), in_=w1_words[0].rearrange("p n t -> p (n t)").bitcast(I32))

@@ -25,10 +25,11 @@ PSUM_BANKS = 8
 
 ON_VECTOR = S // 2
 
-PLAIN_PARTS = [[], [], [192], [UNIT, UNIT]]
+PLAIN = [0, 0, 192, 192]
+HEAD = 2 * UNIT
 
 LOADS = [
-    [(2048, 1024), (704, 320)],
+    [(1920, 896), (896, 384)],
     [(2048, 896), (768, 384)],
     [(2048, 896), (768, 384)],
     [(2048, 512), (768, 384), (0, 384)],
@@ -86,26 +87,32 @@ def tile_picked_andpool_none_e_kernel(tc, xT, w1_words, w1_scales, offs, out):
                     if width > 0:
                         round_on(out=x16[j][:, c0 : c0 + width], in_=x32[j][:, c0 : c0 + width])
                     c0 = c0 + width
-            e0 = 0
-            for part in PLAIN_PARTS[j]:
-                plain = keep.tile([P, part], BF16, name=f"plain_{j}_{e0}")
-                gather_on_vector(plain[:], j, e0, e0 + part)
-                nc.gpsimd.tensor_copy(out=picked[:, e0 : e0 + part, j], in_=plain[:])
-                e0 = e0 + part
-            gather_on_vector(picked[:, e0:ON_VECTOR, j], j, e0, ON_VECTOR)
+            head = PLAIN[j]
+            if head > 0:
+                plain = keep.tile([P, head], BF16, name=f"plain_{j}", tag=f"plain_{j}", align_bytes=64)
+                gather_on_vector(plain[:], j, 0, head)
+                nc.gpsimd.tensor_copy(out=picked[:, :head, j], in_=plain[:])
+            gather_on_vector(picked[:, head:ON_VECTOR, j], j, head, ON_VECTOR)
             gather_on_scalar(picked[:, ON_VECTOR:, j], j, ON_VECTOR, S)
 
         nc.sync.dma_start(out=w_codes[:].bitcast(I32), in_=w1_words[0].rearrange("p n t -> p (n t)").bitcast(I32))
         for q in range(P // 32):
             nc.sync.dma_start(out=w_scales[32 * q : 32 * q + 4, :].bitcast(I32), in_=w1_scales[0, 4 * q : 4 * q + 4, :].bitcast(I32))
 
-        x_codes = keep.tile([P, S], U32, name="x_codes", align_bytes=64)
+        shares_of_list = [(0, HEAD, "head_codes"), (HEAD, ON_VECTOR, f"plain_{PACK - 1}"), (ON_VECTOR, S, "scalar_codes")]
+        code_tiles = [keep.tile([P, e1 - e0], U32, name=f"codes_{e0}", tag=tag, align_bytes=64) for e0, e1, tag in shares_of_list]
+
+        def x_codes(entries):
+            for (e0, e1, tag), codes in zip(shares_of_list, code_tiles):
+                if e0 <= entries.start < e1:
+                    return codes[:, entries.start - e0 : entries.stop - e0].bitcast(FP8X4)
+
         x_scales = keep.tile([P, S], U8, name="x_scales", align_bytes=64)
         e0 = 0
         for units in QUANTISE_UNITS:
             e1 = e0 + units * UNIT
             nc.vector.quantize_mx(
-                out=x_codes[:, e0:e1].bitcast(FP8X4),
+                out=x_codes(slice(e0, e1)),
                 scales=x_scales[:, e0:e1],
                 in_=picked[:, e0:e1].rearrange("p n j -> p (n j)"),
             )
@@ -118,7 +125,7 @@ def tile_picked_andpool_none_e_kernel(tc, xT, w1_words, w1_scales, offs, out):
                     out=bank[:, place],
                     lhsT=w_codes[:, h * P : (h + 1) * P].bitcast(FP8X4),
                     lhsT_scale=w_scales[:, h * P : (h + 1) * P],
-                    rhs=x_codes[:, entries].bitcast(FP8X4),
+                    rhs=x_codes(entries),
                     rhs_scale=x_scales[:, entries],
                     start=True,
                     stop=True,

@@ -18,35 +18,25 @@ MULT = mybir.AluOpType.mult
 
 P = 128
 PACK = 4
-UNIT = 128
-RANGES = V // UNIT
+HALVES = N // P
 PER_COLUMN = 16
 PSUM_BANKS = 8
 
-ON_VECTOR = S // 2
-
+ON_VECTOR = 768
 PLAIN = [0, 0, 192, 192]
-HEAD = 2 * UNIT
-
+HEAD = 256
 LOADS = [
     [(1920, 896), (896, 384)],
     [(2048, 896), (768, 384)],
     [(2048, 896), (768, 384)],
     [(2048, 512), (768, 384), (0, 384)],
 ]
-
-QUANTISE_UNITS = [1, 1, 2, 2, 2, 4]
-
-
-def unit_order():
-    order = []
-    for even in range(0, D, 2):
-        for step in range(RANGES + 1):
-            if step < RANGES:
-                order.append((even, step))
-            if step > 0:
-                order.append((even + 1, step - 1))
-    return order
+QUANTISE = [128, 128, 256, 256, 256, 512]
+STEPS = (
+    [(0, 128, (0, 1)), (128, 128, (0, 1))]
+    + [(e, 256, (h,)) for e in range(256, 1280, 256) for h in range(HALVES)]
+    + [(1280, 128, (0, 1)), (1408, 128, (0,)), (1408, 128, (1,))]
+)
 
 
 def tile_picked_andpool_none_e_kernel(tc, xT, w1_words, w1_scales, offs, out):
@@ -70,11 +60,8 @@ def tile_picked_andpool_none_e_kernel(tc, xT, w1_words, w1_scales, offs, out):
         x16 = [keep.tile([P, T], BF16, name=f"x16_{j}") for j in range(PACK)]
         picked = keep.tile([P, S, PACK], BF16, name="picked", align_bytes=64)
 
-        def gather_on_vector(into, j, e0, e1):
-            nc.vector.tensor_copy(out=into, in_=x32[j][:].indirect(offsets[:, e0 // PER_COLUMN : e1 // PER_COLUMN]))
-
-        def gather_on_scalar(into, j, e0, e1):
-            nc.scalar.activation(into, x16[j][:].indirect(offsets[:, e0 // PER_COLUMN : e1 // PER_COLUMN]), COPY)
+        def listed(e0, e1):
+            return offsets[:, e0 // PER_COLUMN : e1 // PER_COLUMN]
 
         for j in range(PACK):
             c0 = 0
@@ -90,63 +77,59 @@ def tile_picked_andpool_none_e_kernel(tc, xT, w1_words, w1_scales, offs, out):
             head = PLAIN[j]
             if head > 0:
                 plain = keep.tile([P, head], BF16, name=f"plain_{j}", tag=f"plain_{j}", align_bytes=64)
-                gather_on_vector(plain[:], j, 0, head)
+                nc.vector.tensor_copy(out=plain[:], in_=x32[j][:].indirect(listed(0, head)))
                 nc.gpsimd.tensor_copy(out=picked[:, :head, j], in_=plain[:])
-            gather_on_vector(picked[:, head:ON_VECTOR, j], j, head, ON_VECTOR)
-            gather_on_scalar(picked[:, ON_VECTOR:, j], j, ON_VECTOR, S)
+            nc.vector.tensor_copy(out=picked[:, head:ON_VECTOR, j], in_=x32[j][:].indirect(listed(head, ON_VECTOR)))
+            nc.scalar.activation(picked[:, ON_VECTOR:, j], x16[j][:].indirect(listed(ON_VECTOR, S)), COPY)
 
         nc.sync.dma_start(out=w_codes[:].bitcast(I32), in_=w1_words[0].rearrange("p n t -> p (n t)").bitcast(I32))
         for q in range(P // 32):
             nc.sync.dma_start(out=w_scales[32 * q : 32 * q + 4, :].bitcast(I32), in_=w1_scales[0, 4 * q : 4 * q + 4, :].bitcast(I32))
 
-        shares_of_list = [(0, HEAD, "head_codes"), (HEAD, ON_VECTOR, f"plain_{PACK - 1}"), (ON_VECTOR, S, "scalar_codes")]
-        code_tiles = [keep.tile([P, e1 - e0], U32, name=f"codes_{e0}", tag=tag, align_bytes=64) for e0, e1, tag in shares_of_list]
+        code_parts = [(0, HEAD, "head_codes"), (HEAD, S // 2, f"plain_{PACK - 1}"), (S // 2, S, "late_codes")]
+        code_tiles = [keep.tile([P, e1 - e0], U32, name=f"codes_{e0}", tag=tag, align_bytes=64) for e0, e1, tag in code_parts]
 
-        def x_codes(entries):
-            for (e0, e1, tag), codes in zip(shares_of_list, code_tiles):
-                if e0 <= entries.start < e1:
-                    return codes[:, entries.start - e0 : entries.stop - e0].bitcast(FP8X4)
+        def x_codes(first, count):
+            for (e0, e1, tag), codes in zip(code_parts, code_tiles):
+                if e0 <= first < e1:
+                    return codes[:, first - e0 : first - e0 + count].bitcast(FP8X4)
 
         x_scales = keep.tile([P, S], U8, name="x_scales", align_bytes=64)
         e0 = 0
-        for units in QUANTISE_UNITS:
-            e1 = e0 + units * UNIT
+        for count in QUANTISE:
             nc.vector.quantize_mx(
-                out=x_codes(slice(e0, e1)),
-                scales=x_scales[:, e0:e1],
-                in_=picked[:, e0:e1].rearrange("p n j -> p (n j)"),
+                out=x_codes(e0, count),
+                scales=x_scales[:, e0 : e0 + count],
+                in_=picked[:, e0 : e0 + count].rearrange("p n j -> p (n j)"),
             )
-            e0 = e1
+            e0 = e0 + count
 
-        def truth_values(into, entries, halves):
-            bank = psum.tile([P, len(halves), UNIT], F32, name="bank", bufs=PSUM_BANKS)
+        truth = keep.tile([P, HALVES, S], F32, name="truth")
+        running = keep.tile([P, HALVES, S], F32, name="running")
+        out_view = out.rearrange("(h p) v -> p h v", p=P)
+        for first, count, halves in STEPS:
+            rows = slice(halves[0], halves[-1] + 1)
+            last = first + count
+            bank = psum.tile([P, len(halves), count], F32, name="bank", bufs=PSUM_BANKS)
             for place, h in enumerate(halves):
                 nc.tensor.matmul_mx(
                     out=bank[:, place],
                     lhsT=w_codes[:, h * P : (h + 1) * P].bitcast(FP8X4),
                     lhsT_scale=w_scales[:, h * P : (h + 1) * P],
-                    rhs=x_codes(entries),
-                    rhs_scale=x_scales[:, entries],
+                    rhs=x_codes(first, count),
+                    rhs_scale=x_scales[:, first:last],
                     start=True,
                     stop=True,
                 )
-            nc.scalar.activation(into, bank[:], SIGMOID)
-
-        out_view = out.rearrange("(h p) v -> p h v", p=P)
-        order = unit_order()
-        so_far = {}
-        for d, r in order:
-            entries = slice(d * V + r * UNIT, d * V + (r + 1) * UNIT)
-            parts = [[0], [1]] if (d, r) == order[-1] else [[0, 1]]
-            for halves in parts:
-                rows = slice(halves[0], halves[-1] + 1)
-                truth = keep.tile([P, len(halves), UNIT], F32, name=f"truth_{d}_{r}_{halves[0]}")
-                truth_values(truth[:], entries, halves)
-                if d == 0:
-                    product = truth
-                else:
-                    product = keep.tile([P, len(halves), UNIT], F32, name=f"product_{d}_{r}_{halves[0]}")
-                    nc.vector.tensor_tensor(product[:], so_far[r][:, rows], truth[:], MULT)
-                if d == D - 1:
-                    nc.sync.dma_start(out=out_view[:, rows, r * UNIT : (r + 1) * UNIT], in_=product[:])
-            so_far[r] = product
+            nc.scalar.activation(truth[:, rows, first:last], bank[:], SIGMOID)
+            begin = max(first, V)
+            if first < V < last:
+                if halves[-1] < HALVES - 1:
+                    continue
+                rows = slice(0, HALVES)
+            if begin < last:
+                before = truth if last <= 2 * V else running
+                nc.vector.tensor_tensor(running[:, rows, begin:last], before[:, rows, begin - V : last - V], truth[:, rows, begin:last], MULT)
+            done = max(first, S - V)
+            if done < last:
+                nc.sync.dma_start(out=out_view[:, rows, done - (S - V) : last - (S - V)], in_=running[:, rows, done:last])

@@ -22,19 +22,13 @@ HALVES = N // P
 PER_COLUMN = 16
 PSUM_BANKS = 8
 
-ON_VECTOR = 768
-PLAIN = [0, 0, 192, 192]
-HEAD = 256
-LOADS = [
-    [(1920, 896), (896, 384)],
-    [(2048, 896), (768, 384)],
-    [(2048, 896), (768, 384)],
-    [(2048, 512), (768, 384), (0, 384)],
-]
-QUANTISE = [128, 128, 256, 256, 256, 512]
+STEPPED = [1024, 512]
+EARLY = (1024, 1536)
+LATE = [(512, 640), (640, 768), (768, 1024), (1280, 1536), (1024, 1280)]
+OWN = (1280, 1536)
 STEPS = (
-    [(0, 128, (0, 1)), (128, 128, (0, 1))]
-    + [(e, 256, (h,)) for e in range(256, 1280, 256) for h in range(HALVES)]
+    [(0, 256, (0, 1)), (256, 256, (0, 1))]
+    + [(e, 256, (h,)) for e in range(512, 1280, 256) for h in range(HALVES)]
     + [(1280, 128, (0, 1)), (1408, 128, (0,)), (1408, 128, (1,))]
 )
 
@@ -57,52 +51,54 @@ def tile_picked_andpool_none_e_kernel(tc, xT, w1_words, w1_scales, offs, out):
 
         planes = xT.rearrange("(p j) t -> p j t", j=PACK)
         x32 = [keep.tile([P, T], F32, name=f"x32_{j}") for j in range(PACK)]
-        x16 = [keep.tile([P, T], BF16, name=f"x16_{j}") for j in range(PACK)]
         picked = keep.tile([P, S, PACK], BF16, name="picked", align_bytes=64)
+        plain = {}
+        for pair, parts in enumerate([[EARLY], LATE]):
+            for e0, e1 in parts:
+                plain[pair, e0] = keep.tile([P, 2, e1 - e0], BF16, name=f"plain_{pair}_{e0}", align_bytes=64)
 
         def listed(e0, e1):
             return offsets[:, e0 // PER_COLUMN : e1 // PER_COLUMN]
 
+        def lay_in(copy, pair, e0, e1):
+            copy(out=picked[:, e0:e1, 2 * pair : 2 * pair + 2], in_=plain[pair, e0][:].rearrange("p j n -> p n j"))
+
         for j in range(PACK):
-            c0 = 0
-            for shares in LOADS[j]:
-                c1 = c0 + sum(shares)
-                nc.sync.dma_start(out=x32[j][:, c0:c1], in_=planes[:, j, c0:c1])
-                if j == 0 and c0 == 0:
-                    nc.sync.dma_start(offsets[:], offs)
-                for round_on, width in zip((nc.vector.tensor_copy, nc.scalar.copy), shares):
-                    if width > 0:
-                        round_on(out=x16[j][:, c0 : c0 + width], in_=x32[j][:, c0 : c0 + width])
-                    c0 = c0 + width
-            head = PLAIN[j]
-            if head > 0:
-                plain = keep.tile([P, head], BF16, name=f"plain_{j}", tag=f"plain_{j}", align_bytes=64)
-                nc.vector.tensor_copy(out=plain[:], in_=x32[j][:].indirect(listed(0, head)))
-                nc.gpsimd.tensor_copy(out=picked[:, :head, j], in_=plain[:])
-            nc.vector.tensor_copy(out=picked[:, head:ON_VECTOR, j], in_=x32[j][:].indirect(listed(head, ON_VECTOR)))
-            nc.scalar.activation(picked[:, ON_VECTOR:, j], x16[j][:].indirect(listed(ON_VECTOR, S)), COPY)
+            pair = j // 2
+            nc.sync.dma_start(out=x32[j][:], in_=planes[:, j, :])
+            if j == 0:
+                nc.sync.dma_start(offsets[:], offs)
+            nc.vector.tensor_copy(out=picked[:, : STEPPED[pair], j], in_=x32[j][:].indirect(listed(0, STEPPED[pair])))
+            for e0, e1 in [[EARLY], LATE][pair]:
+                nc.scalar.activation(plain[pair, e0][:, j % 2, :], x32[j][:].indirect(listed(e0, e1)), COPY)
+            if j == 1:
+                lay_in(nc.scalar.copy, 0, *EARLY)
+        lay_in(nc.scalar.copy, 1, *OWN)
 
         nc.sync.dma_start(out=w_codes[:].bitcast(I32), in_=w1_words[0].rearrange("p n t -> p (n t)").bitcast(I32))
         for q in range(P // 32):
             nc.sync.dma_start(out=w_scales[32 * q : 32 * q + 4, :].bitcast(I32), in_=w1_scales[0, 4 * q : 4 * q + 4, :].bitcast(I32))
 
-        code_parts = [(0, HEAD, "head_codes"), (HEAD, S // 2, f"plain_{PACK - 1}"), (S // 2, S, "late_codes")]
-        code_tiles = [keep.tile([P, e1 - e0], U32, name=f"codes_{e0}", tag=tag, align_bytes=64) for e0, e1, tag in code_parts]
-
-        def x_codes(first, count):
-            for (e0, e1, tag), codes in zip(code_parts, code_tiles):
-                if e0 <= first < e1:
-                    return codes[:, first - e0 : first - e0 + count].bitcast(FP8X4)
-
+        x_codes = keep.tile([P, S], U32, name="x_codes", align_bytes=64)
         x_scales = keep.tile([P, S], U8, name="x_scales", align_bytes=64)
-        e0 = 0
-        for count in QUANTISE:
+
+        def quantise(e0, e1):
             nc.vector.quantize_mx(
-                out=x_codes(e0, count),
-                scales=x_scales[:, e0 : e0 + count],
-                in_=picked[:, e0 : e0 + count].rearrange("p n j -> p (n j)"),
+                out=x_codes[:, e0:e1].bitcast(FP8X4),
+                scales=x_scales[:, e0:e1],
+                in_=picked[:, e0:e1].rearrange("p n j -> p (n j)"),
             )
-            e0 = e0 + count
+
+        lay_in(nc.vector.tensor_copy, 1, 512, 640)
+        quantise(0, 256)
+        quantise(256, 512)
+        lay_in(nc.vector.tensor_copy, 1, 640, 768)
+        lay_in(nc.vector.tensor_copy, 1, 768, 1024)
+        quantise(512, 768)
+        lay_in(nc.vector.tensor_copy, 1, 1024, 1280)
+        quantise(768, 1024)
+        quantise(1280, 1536)
+        quantise(1024, 1280)
 
         truth = keep.tile([P, HALVES, S], F32, name="truth")
         running = keep.tile([P, HALVES, S], F32, name="running")
@@ -116,17 +112,13 @@ def tile_picked_andpool_none_e_kernel(tc, xT, w1_words, w1_scales, offs, out):
                     out=bank[:, place],
                     lhsT=w_codes[:, h * P : (h + 1) * P].bitcast(FP8X4),
                     lhsT_scale=w_scales[:, h * P : (h + 1) * P],
-                    rhs=x_codes(first, count),
+                    rhs=x_codes[:, first:last].bitcast(FP8X4),
                     rhs_scale=x_scales[:, first:last],
                     start=True,
                     stop=True,
                 )
             nc.scalar.activation(truth[:, rows, first:last], bank[:], SIGMOID)
             begin = max(first, V)
-            if first < V < last:
-                if halves[-1] < HALVES - 1:
-                    continue
-                rows = slice(0, HALVES)
             if begin < last:
                 before = truth if last <= 2 * V else running
                 nc.vector.tensor_tensor(running[:, rows, begin:last], before[:, rows, begin - V : last - V], truth[:, rows, begin:last], MULT)

@@ -22,10 +22,10 @@ HALVES = N // P
 PER_COLUMN = 16
 PSUM_BANKS = 8
 
-STEPPED = [1024, 512]
-EARLY = (1024, 1536)
-LATE = [(512, 640), (640, 768), (768, 1024), (1280, 1536), (1024, 1280)]
-OWN = (1280, 1536)
+STEPPED = [(704, 1536), (0, 512)]
+EARLY = (0, 704)
+LATE = [(512, 704), (704, 896), (896, 1088), (1312, 1536), (1088, 1312)]
+OWN = (1312, 1536)
 STEPS = (
     [(0, 256, (0, 1)), (256, 256, (0, 1))]
     + [(e, 256, (h,)) for e in range(512, 1280, 256) for h in range(HALVES)]
@@ -50,12 +50,13 @@ def tile_picked_andpool_none_e_kernel(tc, xT, w1_words, w1_scales, offs, out):
         nc.scalar.activation(warm_out[:], warm[:], SIGMOID)
 
         planes = xT.rearrange("(p j) t -> p j t", j=PACK)
-        x32 = [keep.tile([P, T], F32, name=f"x32_{j}") for j in range(PACK)]
+        first_pair = keep.tile([P, 2, T], F32, name="first_pair")
+        x32 = [first_pair[:, 0], first_pair[:, 1]] + [keep.tile([P, T], F32, name=f"x32_{j}")[:] for j in (2, 3)]
         picked = keep.tile([P, S, PACK], BF16, name="picked", align_bytes=64)
         plain = {}
         for pair, parts in enumerate([[EARLY], LATE]):
             for e0, e1 in parts:
-                plain[pair, e0] = keep.tile([P, 2, e1 - e0], BF16, name=f"plain_{pair}_{e0}", align_bytes=64)
+                plain[pair, e0] = keep.tile([P, 2, e1 - e0], [F32, BF16][pair], name=f"plain_{pair}_{e0}", align_bytes=64)
 
         def listed(e0, e1):
             return offsets[:, e0 // PER_COLUMN : e1 // PER_COLUMN]
@@ -65,14 +66,18 @@ def tile_picked_andpool_none_e_kernel(tc, xT, w1_words, w1_scales, offs, out):
 
         for j in range(PACK):
             pair = j // 2
-            nc.sync.dma_start(out=x32[j][:], in_=planes[:, j, :])
             if j == 0:
+                nc.sync.dma_start(out=first_pair[:], in_=planes[:, 0:2, :])
                 nc.sync.dma_start(offsets[:], offs)
-            nc.vector.tensor_copy(out=picked[:, : STEPPED[pair], j], in_=x32[j][:].indirect(listed(0, STEPPED[pair])))
+            if pair == 1:
+                nc.sync.dma_start(out=x32[j], in_=planes[:, j, :])
+            e0, e1 = STEPPED[pair]
+            nc.vector.tensor_copy(out=picked[:, e0:e1, j], in_=x32[j].indirect(listed(e0, e1)))
             for e0, e1 in [[EARLY], LATE][pair]:
-                nc.scalar.activation(plain[pair, e0][:, j % 2, :], x32[j][:].indirect(listed(e0, e1)), COPY)
+                nc.scalar.activation(plain[pair, e0][:, j % 2, :], x32[j].indirect(listed(e0, e1)), COPY)
             if j == 1:
                 lay_in(nc.scalar.copy, 0, *EARLY)
+        lay_in(nc.gpsimd.tensor_copy, 1, *LATE[0])
         lay_in(nc.scalar.copy, 1, *OWN)
 
         nc.sync.dma_start(out=w_codes[:].bitcast(I32), in_=w1_words[0].rearrange("p n t -> p (n t)").bitcast(I32))
@@ -89,16 +94,15 @@ def tile_picked_andpool_none_e_kernel(tc, xT, w1_words, w1_scales, offs, out):
                 in_=picked[:, e0:e1].rearrange("p n j -> p (n j)"),
             )
 
-        lay_in(nc.vector.tensor_copy, 1, 512, 640)
+        lay_in(nc.vector.tensor_copy, 1, 704, 896)
         quantise(0, 256)
         quantise(256, 512)
-        lay_in(nc.vector.tensor_copy, 1, 640, 768)
-        lay_in(nc.vector.tensor_copy, 1, 768, 1024)
+        lay_in(nc.vector.tensor_copy, 1, 896, 1088)
         quantise(512, 768)
-        lay_in(nc.vector.tensor_copy, 1, 1024, 1280)
+        lay_in(nc.vector.tensor_copy, 1, 1088, 1312)
         quantise(768, 1024)
-        quantise(1280, 1536)
         quantise(1024, 1280)
+        quantise(1280, 1536)
 
         truth = keep.tile([P, HALVES, S], F32, name="truth")
         running = keep.tile([P, HALVES, S], F32, name="running")

@@ -56,7 +56,7 @@ def tile_picked_andpool_none_e_kernel(tc, xT, w1_words, w1_scales, offs, out):
         plain = {}
         for pair, parts in enumerate([[EARLY], LATE]):
             for e0, e1 in parts:
-                plain[pair, e0] = keep.tile([P, 2, e1 - e0], [F32, BF16][pair], name=f"plain_{pair}_{e0}", align_bytes=64)
+                plain[pair, e0] = keep.tile([P, 2, e1 - e0], [F32, BF16][pair], name=f"plain_{pair}_{e0}", tag=f"plain_{pair}_{e0}", align_bytes=64)
 
         def listed(e0, e1):
             return offsets[:, e0 // PER_COLUMN : e1 // PER_COLUMN]
@@ -75,21 +75,30 @@ def tile_picked_andpool_none_e_kernel(tc, xT, w1_words, w1_scales, offs, out):
             nc.vector.tensor_copy(out=picked[:, e0:e1, j], in_=x32[j].indirect(listed(e0, e1)))
             for e0, e1 in [[EARLY], LATE][pair]:
                 nc.scalar.activation(plain[pair, e0][:, j % 2, :], x32[j].indirect(listed(e0, e1)), COPY)
+            if pair == 1:
+                e0, e1 = LATE[0]
+                nc.gpsimd.tensor_copy(out=picked[:, e0:e1, j], in_=plain[1, e0][:, j % 2, :])
             if j == 1:
                 lay_in(nc.scalar.copy, 0, *EARLY)
-        lay_in(nc.gpsimd.tensor_copy, 1, *LATE[0])
         lay_in(nc.scalar.copy, 1, *OWN)
 
         nc.sync.dma_start(out=w_codes[:].bitcast(I32), in_=w1_words[0].rearrange("p n t -> p (n t)").bitcast(I32))
         for q in range(P // 32):
             nc.sync.dma_start(out=w_scales[32 * q : 32 * q + 4, :].bitcast(I32), in_=w1_scales[0, 4 * q : 4 * q + 4, :].bitcast(I32))
 
-        x_codes = keep.tile([P, S], U32, name="x_codes", align_bytes=64)
+        stepped = STEPPED[1][1]
+        head_codes = keep.tile([P, stepped], U32, name="head_codes", tag=f"plain_1_{LATE[0][0]}", align_bytes=64)
+        tail_codes = keep.tile([P, S - stepped], U32, name="tail_codes", align_bytes=64)
+
+        def x_codes(e0, e1):
+            codes = head_codes[:, e0:e1] if e0 < stepped else tail_codes[:, e0 - stepped : e1 - stepped]
+            return codes.bitcast(FP8X4)
+
         x_scales = keep.tile([P, S], U8, name="x_scales", align_bytes=64)
 
         def quantise(e0, e1):
             nc.vector.quantize_mx(
-                out=x_codes[:, e0:e1].bitcast(FP8X4),
+                out=x_codes(e0, e1),
                 scales=x_scales[:, e0:e1],
                 in_=picked[:, e0:e1].rearrange("p n j -> p (n j)"),
             )
@@ -116,7 +125,7 @@ def tile_picked_andpool_none_e_kernel(tc, xT, w1_words, w1_scales, offs, out):
                     out=bank[:, place],
                     lhsT=w_codes[:, h * P : (h + 1) * P].bitcast(FP8X4),
                     lhsT_scale=w_scales[:, h * P : (h + 1) * P],
-                    rhs=x_codes[:, first:last].bitcast(FP8X4),
+                    rhs=x_codes(first, last),
                     rhs_scale=x_scales[:, first:last],
                     start=True,
                     stop=True,

@@ -24,11 +24,11 @@ PSUM_BANKS = 8
 
 STEPPED = [(704, 1536), (0, 512)]
 EARLY = (0, 704)
-LATE = [(512, 704), (704, 896), (896, 1088), (1312, 1536), (1088, 1312)]
-OWN = (1312, 1536)
+LATE = [(512, 704), (704, 896), (1344, 1536), (896, 1344)]
+OWN = (1344, 1536)
 STEPS = (
-    [(0, 256, (0, 1)), (256, 256, (0, 1))]
-    + [(e, 256, (h,)) for e in range(512, 1280, 256) for h in range(HALVES)]
+    [(0, 128, (0, 1)), (128, 128, (0, 1)), (256, 256, (0, 1))]
+    + [(e, 128, (0, 1)) for e in range(512, 1280, 128)]
     + [(1280, 128, (0, 1)), (1408, 128, (0,)), (1408, 128, (1,))]
 )
 
@@ -62,7 +62,9 @@ def tile_picked_andpool_none_e_kernel(tc, xT, w1_words, w1_scales, offs, out):
             return offsets[:, e0 // PER_COLUMN : e1 // PER_COLUMN]
 
         def lay_in(copy, pair, e0, e1):
-            copy(out=picked[:, e0:e1, 2 * pair : 2 * pair + 2], in_=plain[pair, e0][:].rearrange("p j n -> p n j"))
+            start = max(first for which, first in plain if which == pair and first <= e0)
+            part = plain[pair, start][:, :, e0 - start : e1 - start]
+            copy(out=picked[:, e0:e1, 2 * pair : 2 * pair + 2], in_=part.rearrange("p j n -> p n j"))
 
         for j in range(PACK):
             pair = j // 2
@@ -104,14 +106,14 @@ def tile_picked_andpool_none_e_kernel(tc, xT, w1_words, w1_scales, offs, out):
             )
 
         lay_in(nc.vector.tensor_copy, 1, 704, 896)
-        quantise(0, 256)
+        quantise(0, 128)
+        quantise(128, 256)
         quantise(256, 512)
-        lay_in(nc.vector.tensor_copy, 1, 896, 1088)
-        quantise(512, 768)
-        lay_in(nc.vector.tensor_copy, 1, 1088, 1312)
-        quantise(768, 1024)
-        quantise(1024, 1280)
-        quantise(1280, 1536)
+        quantise(512, 896)
+        lay_in(nc.vector.tensor_copy, 1, 896, 1152)
+        lay_in(nc.vector.tensor_copy, 1, 1152, 1344)
+        quantise(896, 1152)
+        quantise(1152, 1536)
 
         truth = keep.tile([P, HALVES, S], F32, name="truth")
         running = keep.tile([P, HALVES, S], F32, name="running")

@@ -24,12 +24,11 @@ PSUM_BANKS = 8
 
 STEPPED = [(704, 1536), (0, 512)]
 EARLY = (0, 704)
-LATE = [(512, 704), (704, 896), (1344, 1536), (896, 1344)]
-OWN = (1344, 1536)
+LATE = [(512, 704), (704, 896), (1312, 1536), (896, 1312)]
+OWN = (1312, 1536)
 STEPS = (
-    [(0, 128, (0, 1)), (128, 128, (0, 1)), (256, 256, (0, 1))]
-    + [(e, 128, (0, 1)) for e in range(512, 1280, 128)]
-    + [(1280, 128, (0, 1)), (1408, 128, (0,)), (1408, 128, (1,))]
+    [(e, 128, (0, 1)) for e in range(0, 1408, 128)]
+    + [(1408, 128, (0,)), (1408, 128, (1,))]
 )
 
 
@@ -111,7 +110,7 @@ def tile_picked_andpool_none_e_kernel(tc, xT, w1_words, w1_scales, offs, out):
         quantise(256, 512)
         quantise(512, 896)
         lay_in(nc.vector.tensor_copy, 1, 896, 1152)
-        lay_in(nc.vector.tensor_copy, 1, 1152, 1344)
+        lay_in(nc.vector.tensor_copy, 1, 1152, 1312)
         quantise(896, 1152)
         quantise(1152, 1536)
 

@@ -22,8 +22,8 @@ HALVES = N // P
 PER_COLUMN = 16
 PSUM_BANKS = 8
 
-STEPPED = [(704, 1536), (0, 512)]
-EARLY = (0, 704)
+STEPPED = [(736, 1536), (0, 512)]
+EARLY = (0, 736)
 LATE = [(512, 704), (704, 896), (1312, 1536), (896, 1312)]
 OWN = (1312, 1536)
 STEPS = (
@@ -80,7 +80,9 @@ def tile_picked_andpool_none_e_kernel(tc, xT, w1_words, w1_scales, offs, out):
                 e0, e1 = LATE[0]
                 nc.gpsimd.tensor_copy(out=picked[:, e0:e1, j], in_=plain[1, e0][:, j % 2, :])
             if j == 1:
-                lay_in(nc.scalar.copy, 0, *EARLY)
+                lay_in(nc.gpsimd.tensor_copy, 0, *LATE[0])
+                lay_in(nc.scalar.copy, 0, EARLY[0], LATE[0][0])
+                lay_in(nc.scalar.copy, 0, LATE[0][1], EARLY[1])
         lay_in(nc.scalar.copy, 1, *OWN)
 
         nc.sync.dma_start(out=w_codes[:].bitcast(I32), in_=w1_words[0].rearrange("p n t -> p (n t)").bitcast(I32))

@@ -26,6 +26,7 @@ STEPPED = [(736, 1536), (0, 512)]
 EARLY = (0, 736)
 LATE = [(512, 704), (704, 896), (1312, 1536), (896, 1312)]
 OWN = (1312, 1536)
+SCALE_LOADS = [(0, 4)] + [(row, 2) for row in range(4, 16, 2)]
 STEPS = (
     [(e, 128, (0, 1)) for e in range(0, 1408, 128)]
     + [(1408, 128, (0,)), (1408, 128, (1,))]
@@ -85,9 +86,10 @@ def tile_picked_andpool_none_e_kernel(tc, xT, w1_words, w1_scales, offs, out):
                 lay_in(nc.scalar.copy, 0, LATE[0][1], EARLY[1])
         lay_in(nc.scalar.copy, 1, *OWN)
 
+        for row, count in SCALE_LOADS:
+            first = 32 * (row // 4) + row % 4
+            nc.sync.dma_start(out=w_scales[first : first + count, :].bitcast(I32), in_=w1_scales[0, row : row + count, :].bitcast(I32))
         nc.sync.dma_start(out=w_codes[:].bitcast(I32), in_=w1_words[0].rearrange("p n t -> p (n t)").bitcast(I32))
-        for q in range(P // 32):
-            nc.sync.dma_start(out=w_scales[32 * q : 32 * q + 4, :].bitcast(I32), in_=w1_scales[0, 4 * q : 4 * q + 4, :].bitcast(I32))
 
         stepped = STEPPED[1][1]
         head_codes = keep.tile([P, stepped], U32, name="head_codes", tag=f"plain_1_{LATE[0][0]}", align_bytes=64)

@@ -22,10 +22,11 @@ HALVES = N // P
 PER_COLUMN = 16
 PSUM_BANKS = 8
 
-STEPPED = [(736, 1536), (0, 512)]
-EARLY = (0, 736)
-LATE = [(512, 704), (704, 896), (1312, 1536), (896, 1312)]
-OWN = (1312, 1536)
+GPSIMD = [(0, 64), (64, 320)]
+STEPPED = (320, 896)
+OWN = [(896, 1152)]
+LAID = [(1152, 1536)]
+EARLY_SPLIT = 1120
 SCALE_LOADS = [(0, 4)] + [(row, 2) for row in range(4, 16, 2)]
 STEPS = (
     [(e, 128, (0, 1)) for e in range(0, 1408, 128)]
@@ -50,71 +51,76 @@ def tile_picked_andpool_none_e_kernel(tc, xT, w1_words, w1_scales, offs, out):
         nc.scalar.activation(warm_out[:], warm[:], SIGMOID)
 
         planes = xT.rearrange("(p j) t -> p j t", j=PACK)
-        first_pair = keep.tile([P, 2, T], F32, name="first_pair")
-        x32 = [first_pair[:, 0], first_pair[:, 1]] + [keep.tile([P, T], F32, name=f"x32_{j}")[:] for j in (2, 3)]
         picked = keep.tile([P, S, PACK], BF16, name="picked", align_bytes=64)
-        plain = {}
-        for pair, parts in enumerate([[EARLY], LATE]):
-            for e0, e1 in parts:
-                plain[pair, e0] = keep.tile([P, 2, e1 - e0], [F32, BF16][pair], name=f"plain_{pair}_{e0}", tag=f"plain_{pair}_{e0}", align_bytes=64)
 
         def listed(e0, e1):
             return offsets[:, e0 // PER_COLUMN : e1 // PER_COLUMN]
 
-        def lay_in(copy, pair, e0, e1):
-            start = max(first for which, first in plain if which == pair and first <= e0)
-            part = plain[pair, start][:, :, e0 - start : e1 - start]
+        def gather_at_step(window, j, e0, e1):
+            nc.vector.tensor_copy(out=picked[:, e0:e1, j], in_=window.indirect(listed(e0, e1)))
+
+        def gather_plainly(part, window, e0, e1):
+            nc.scalar.activation(part, window.indirect(listed(e0, e1)), COPY)
+
+        def pair_tile(pair, e0, e1, dtype):
+            return keep.tile([P, 2, e1 - e0], dtype, name=f"plain_{pair}_{e0}", tag=f"plain_{pair}_{e0}", align_bytes=64)
+
+        def lay_in(copy, part, pair, e0, e1):
             copy(out=picked[:, e0:e1, 2 * pair : 2 * pair + 2], in_=part.rearrange("p j n -> p n j"))
 
-        for j in range(PACK):
-            pair = j // 2
-            if j == 0:
-                nc.sync.dma_start(out=first_pair[:], in_=planes[:, 0:2, :])
-                nc.sync.dma_start(offsets[:], offs)
-            if pair == 1:
-                nc.sync.dma_start(out=x32[j], in_=planes[:, j, :])
-            e0, e1 = STEPPED[pair]
-            nc.vector.tensor_copy(out=picked[:, e0:e1, j], in_=x32[j].indirect(listed(e0, e1)))
-            for e0, e1 in [[EARLY], LATE][pair]:
-                nc.scalar.activation(plain[pair, e0][:, j % 2, :], x32[j].indirect(listed(e0, e1)), COPY)
-            if pair == 1:
-                e0, e1 = LATE[0]
-                nc.gpsimd.tensor_copy(out=picked[:, e0:e1, j], in_=plain[1, e0][:, j % 2, :])
-            if j == 1:
-                lay_in(nc.gpsimd.tensor_copy, 0, *LATE[0])
-                lay_in(nc.scalar.copy, 0, EARLY[0], LATE[0][0])
-                lay_in(nc.scalar.copy, 0, LATE[0][1], EARLY[1])
-        lay_in(nc.scalar.copy, 1, *OWN)
+        first_pair = keep.tile([P, 2, T], F32, name="first_pair")
+        nc.sync.dma_start(out=first_pair[:], in_=planes[:, 0:2, :])
+        nc.sync.dma_start(offsets[:], offs)
+        early = [((0, STEPPED[0]), nc.gpsimd.tensor_copy), ((EARLY_SPLIT, S), nc.scalar.copy)]
+        early_tiles = [pair_tile(0, *part, F32) for part, copy in early]
+        for j in range(2):
+            gather_at_step(first_pair[:, j], j, STEPPED[0], EARLY_SPLIT)
+            for (part, copy), plain in zip(early, early_tiles):
+                gather_plainly(plain[:, j, :], first_pair[:, j], *part)
+        for (part, copy), plain in zip(early, early_tiles):
+            lay_in(copy, plain[:], 0, *part)
+
+        for_gpsimd = [pair_tile(1, *part, F32) for part in GPSIMD]
+        own = [pair_tile(1, *part, BF16) for part in OWN]
+        laid = [pair_tile(1, *part, BF16) for part in LAID]
+        for j in (2, 3):
+            plane = keep.tile([P, T], F32, name=f"x32_{j}")
+            nc.sync.dma_start(out=plane[:], in_=planes[:, j, :])
+            gather_at_step(plane[:], j, *STEPPED)
+            for (e0, e1), plain in zip(GPSIMD, for_gpsimd):
+                gather_plainly(plain[:, j % 2, :], plane[:], e0, e1)
+                nc.gpsimd.tensor_copy(out=picked[:, e0:e1, j], in_=plain[:, j % 2, :])
+            for part, plain in zip(OWN, own):
+                gather_plainly(plain[:, j % 2, :], plane[:], *part)
+            if j == 3:
+                for part, plain in zip(OWN, own):
+                    lay_in(nc.scalar.copy, plain[:], 1, *part)
+            for part, plain in zip(LAID, laid):
+                gather_plainly(plain[:, j % 2, :], plane[:], *part)
 
         for row, count in SCALE_LOADS:
             first = 32 * (row // 4) + row % 4
             nc.sync.dma_start(out=w_scales[first : first + count, :].bitcast(I32), in_=w1_scales[0, row : row + count, :].bitcast(I32))
         nc.sync.dma_start(out=w_codes[:].bitcast(I32), in_=w1_words[0].rearrange("p n t -> p (n t)").bitcast(I32))
 
-        stepped = STEPPED[1][1]
-        head_codes = keep.tile([P, stepped], U32, name="head_codes", tag=f"plain_1_{LATE[0][0]}", align_bytes=64)
-        tail_codes = keep.tile([P, S - stepped], U32, name="tail_codes", align_bytes=64)
+        head = STEPPED[1]
+        head_codes = keep.tile([P, head], U32, name="head_codes", tag=f"plain_1_{GPSIMD[-1][0]}", align_bytes=64)
+        tail_codes = keep.tile([P, S - head], U32, name="tail_codes", align_bytes=64)
 
         def x_codes(e0, e1):
-            codes = head_codes[:, e0:e1] if e0 < stepped else tail_codes[:, e0 - stepped : e1 - stepped]
+            codes = head_codes[:, e0:e1] if e0 < head else tail_codes[:, e0 - head : e1 - head]
             return codes.bitcast(FP8X4)
 
         x_scales = keep.tile([P, S], U8, name="x_scales", align_bytes=64)
 
         def quantise(e0, e1):
-            nc.vector.quantize_mx(
-                out=x_codes(e0, e1),
-                scales=x_scales[:, e0:e1],
-                in_=picked[:, e0:e1].rearrange("p n j -> p (n j)"),
-            )
+            nc.vector.quantize_mx(out=x_codes(e0, e1), scales=x_scales[:, e0:e1], in_=picked[:, e0:e1].rearrange("p n j -> p (n j)"))
 
-        lay_in(nc.vector.tensor_copy, 1, 704, 896)
         quantise(0, 128)
         quantise(128, 256)
         quantise(256, 512)
         quantise(512, 896)
-        lay_in(nc.vector.tensor_copy, 1, 896, 1152)
-        lay_in(nc.vector.tensor_copy, 1, 1152, 1312)
+        lay_in(nc.vector.tensor_copy, laid[0][:], 1, *LAID[0])
         quantise(896, 1152)
         quantise(1152, 1536)
 

@@ -22,11 +22,11 @@ HALVES = N // P
 PER_COLUMN = 16
 PSUM_BANKS = 8
 
-GPSIMD = [(0, 64), (64, 320)]
-STEPPED = (320, 896)
-OWN = [(896, 1152)]
-LAID = [(1152, 1536)]
-EARLY_SPLIT = 1120
+GPSIMD = [(0, 128), (128, 256)]
+STEPPED = (256, 832)
+OWN = [(832, 1120)]
+LAID = [(1120, 1536)]
+EARLY_SPLIT = 1056
 SCALE_LOADS = [(0, 4)] + [(row, 2) for row in range(4, 16, 2)]
 STEPS = (
     [(e, 128, (0, 1)) for e in range(0, 1408, 128)]
@@ -80,7 +80,7 @@ def tile_picked_andpool_none_e_kernel(tc, xT, w1_words, w1_scales, offs, out):
         for (part, copy), plain in zip(early, early_tiles):
             lay_in(copy, plain[:], 0, *part)
 
-        for_gpsimd = [pair_tile(1, *part, F32) for part in GPSIMD]
+        for_gpsimd = [pair_tile(1, *part, BF16) for part in GPSIMD]
         own = [pair_tile(1, *part, BF16) for part in OWN]
         laid = [pair_tile(1, *part, BF16) for part in LAID]
         for j in (2, 3):
@@ -103,7 +103,7 @@ def tile_picked_andpool_none_e_kernel(tc, xT, w1_words, w1_scales, offs, out):
             nc.sync.dma_start(out=w_scales[first : first + count, :].bitcast(I32), in_=w1_scales[0, row : row + count, :].bitcast(I32))
         nc.sync.dma_start(out=w_codes[:].bitcast(I32), in_=w1_words[0].rearrange("p n t -> p (n t)").bitcast(I32))
 
-        head = STEPPED[1]
+        head = 768
         head_codes = keep.tile([P, head], U32, name="head_codes", tag=f"plain_1_{GPSIMD[-1][0]}", align_bytes=64)
         tail_codes = keep.tile([P, S - head], U32, name="tail_codes", align_bytes=64)
 
@@ -119,10 +119,10 @@ def tile_picked_andpool_none_e_kernel(tc, xT, w1_words, w1_scales, offs, out):
         quantise(0, 128)
         quantise(128, 256)
         quantise(256, 512)
-        quantise(512, 896)
+        quantise(512, 768)
         lay_in(nc.vector.tensor_copy, laid[0][:], 1, *LAID[0])
-        quantise(896, 1152)
-        quantise(1152, 1536)
+        quantise(768, 1024)
+        quantise(1024, 1536)
 
         truth = keep.tile([P, HALVES, S], F32, name="truth")
         running = keep.tile([P, HALVES, S], F32, name="running")

@@ -24,8 +24,8 @@ PSUM_BANKS = 8
 
 GPSIMD = [(0, 128), (128, 256)]
 STEPPED = (256, 832)
-OWN = [(832, 1120)]
-LAID = [(1120, 1536)]
+OWN = [(832, 1088)]
+LAID = [(1088, 1536)]
 EARLY_SPLIT = 1056
 SCALE_LOADS = [(0, 4)] + [(row, 2) for row in range(4, 16, 2)]
 STEPS = (

@@ -22,11 +22,11 @@ HALVES = N // P
 PER_COLUMN = 16
 PSUM_BANKS = 8
 
-GPSIMD = [(0, 128), (128, 256)]
-STEPPED = (256, 832)
-OWN = [(832, 1088)]
+GPSIMD = [(0, 128), (128, 288)]
+STEPPED = (288, 864)
+OWN = [(864, 1088)]
 LAID = [(1088, 1536)]
-EARLY_SPLIT = 1056
+EARLY_SPLIT = 1088
 SCALE_LOADS = [(0, 4)] + [(row, 2) for row in range(4, 16, 2)]
 STEPS = (
     [(e, 128, (0, 1)) for e in range(0, 1408, 128)]

from contextlib import ExitStack

import concourse.mybir as mybir

K, T, S, V, N, D = 512, 4096, 1536, 384, 256, 4
FLOPS = 2 * K * N * S

F32 = mybir.dt.float32
BF16 = mybir.dt.bfloat16
I32 = mybir.dt.int32
U32 = mybir.dt.uint32
U16 = mybir.dt.uint16
U8 = mybir.dt.uint8
FP8X4 = mybir.dt.float8_e4m3fn_x4
COPY = mybir.ActivationFunctionType.Copy
SIGMOID = mybir.ActivationFunctionType.Sigmoid
MULT = mybir.AluOpType.mult

P = 128
PACK = 4
HALVES = N // P
PER_COLUMN = 16
PSUM_BANKS = 8

GPSIMD = [(0, 128), (128, 288)]
STEPPED = (288, 864)
OWN = [(864, 1088)]
LAID = [(1088, 1536)]
EARLY_SPLIT = 1088
SCALE_LOADS = [(0, 4)] + [(row, 2) for row in range(4, 16, 2)]
STEPS = (
    [(e, 128, (0, 1)) for e in range(0, 1408, 128)]
    + [(1408, 128, (0,)), (1408, 128, (1,))]
)


def tile_picked_andpool_none_e_kernel(tc, xT, w1_words, w1_scales, offs, out):
    nc = tc.nc
    with ExitStack() as ctx:
        keep = ctx.enter_context(tc.tile_pool(name="keep", bufs=1))
        psum = ctx.enter_context(tc.psum_pool(name="psum", bufs=1))

        offsets = keep.tile([P, S // PER_COLUMN], U16, name="offsets")
        w_codes = keep.tile([P, N], U32, name="w_codes", align_bytes=64)
        w_scales = keep.tile([P, N], U8, name="w_scales", align_bytes=64)
        nc.vector.memset(w_scales[:].bitcast(I32), 0)

        warm = keep.tile([P, 1], F32, name="warm")
        warm_out = keep.tile([P, 1], F32, name="warm_out")
        nc.vector.memset(warm[:], 0.0)
        nc.scalar.activation(warm_out[:], warm[:], SIGMOID)

        planes = xT.rearrange("(p j) t -> p j t", j=PACK)
        picked = keep.tile([P, S, PACK], BF16, name="picked", align_bytes=64)

        def listed(e0, e1):
            return offsets[:, e0 // PER_COLUMN : e1 // PER_COLUMN]

        def gather_at_step(window, j, e0, e1):
            nc.vector.tensor_copy(out=picked[:, e0:e1, j], in_=window.indirect(listed(e0, e1)))

        def gather_plainly(part, window, e0, e1):
            nc.scalar.activation(part, window.indirect(listed(e0, e1)), COPY)

        def pair_tile(pair, e0, e1, dtype):
            return keep.tile([P, 2, e1 - e0], dtype, name=f"plain_{pair}_{e0}", tag=f"plain_{pair}_{e0}", align_bytes=64)

        def lay_in(copy, part, pair, e0, e1):
            copy(out=picked[:, e0:e1, 2 * pair : 2 * pair + 2], in_=part.rearrange("p j n -> p n j"))

        first_pair = keep.tile([P, 2, T], F32, name="first_pair")
        nc.sync.dma_start(out=first_pair[:], in_=planes[:, 0:2, :])
        nc.sync.dma_start(offsets[:], offs)
        early = [((0, STEPPED[0]), nc.gpsimd.tensor_copy), ((EARLY_SPLIT, S), nc.scalar.copy)]
        early_tiles = [pair_tile(0, *part, F32) for part, copy in early]
        for j in range(2):
            gather_at_step(first_pair[:, j], j, STEPPED[0], EARLY_SPLIT)
            for (part, copy), plain in zip(early, early_tiles):
                gather_plainly(plain[:, j, :], first_pair[:, j], *part)
        for (part, copy), plain in zip(early, early_tiles):
            lay_in(copy, plain[:], 0, *part)

        for_gpsimd = [pair_tile(1, *part, BF16) for part in GPSIMD]
        own = [pair_tile(1, *part, BF16) for part in OWN]
        laid = [pair_tile(1, *part, BF16) for part in LAID]
        for j in (2, 3):
            plane = keep.tile([P, T], F32, name=f"x32_{j}")
            nc.sync.dma_start(out=plane[:], in_=planes[:, j, :])
            gather_at_step(plane[:], j, *STEPPED)
            for (e0, e1), plain in zip(GPSIMD, for_gpsimd):
                gather_plainly(plain[:, j % 2, :], plane[:], e0, e1)
                nc.gpsimd.tensor_copy(out=picked[:, e0:e1, j], in_=plain[:, j % 2, :])
            for part, plain in zip(OWN, own):
                gather_plainly(plain[:, j % 2, :], plane[:], *part)
            if j == 3:
                for part, plain in zip(OWN, own):
                    lay_in(nc.scalar.copy, plain[:], 1, *part)
            for part, plain in zip(LAID, laid):
                gather_plainly(plain[:, j % 2, :], plane[:], *part)

        for row, count in SCALE_LOADS:
            first = 32 * (row // 4) + row % 4
            nc.sync.dma_start(out=w_scales[first : first + count, :].bitcast(I32), in_=w1_scales[0, row : row + count, :].bitcast(I32))
        nc.sync.dma_start(out=w_codes[:].bitcast(I32), in_=w1_words[0].rearrange("p n t -> p (n t)").bitcast(I32))

        head = 768
        head_codes = keep.tile([P, head], U32, name="head_codes", tag=f"plain_1_{GPSIMD[-1][0]}", align_bytes=64)
        tail_codes = keep.tile([P, S - head], U32, name="tail_codes", align_bytes=64)

        def x_codes(e0, e1):
            codes = head_codes[:, e0:e1] if e0 < head else tail_codes[:, e0 - head : e1 - head]
            return codes.bitcast(FP8X4)

        x_scales = keep.tile([P, S], U8, name="x_scales", align_bytes=64)

        def quantise(e0, e1):
            nc.vector.quantize_mx(out=x_codes(e0, e1), scales=x_scales[:, e0:e1], in_=picked[:, e0:e1].rearrange("p n j -> p (n j)"))

        quantise(0, 128)
        quantise(128, 256)
        quantise(256, 512)
        quantise(512, 768)
        lay_in(nc.vector.tensor_copy, laid[0][:], 1, *LAID[0])
        quantise(768, 1024)
        quantise(1024, 1536)

        truth = keep.tile([P, HALVES, S], F32, name="truth")
        running = keep.tile([P, HALVES, S], F32, name="running")
        out_view = out.rearrange("(h p) v -> p h v", p=P)
        for first, count, halves in STEPS:
            rows = slice(halves[0], halves[-1] + 1)
            last = first + count
            bank = psum.tile([P, len(halves), count], F32, name="bank", bufs=PSUM_BANKS)
            for place, h in enumerate(halves):
                nc.tensor.matmul_mx(
                    out=bank[:, place],
                    lhsT=w_codes[:, h * P : (h + 1) * P].bitcast(FP8X4),
                    lhsT_scale=w_scales[:, h * P : (h + 1) * P],
                    rhs=x_codes(first, last),
                    rhs_scale=x_scales[:, first:last],
                    start=True,
                    stop=True,
                )
            nc.scalar.activation(truth[:, rows, first:last], bank[:], SIGMOID)
            begin = max(first, V)
            if begin < last:
                before = truth if last <= 2 * V else running
                nc.vector.tensor_tensor(running[:, rows, begin:last], before[:, rows, begin - V : last - V], truth[:, rows, begin:last], MULT)
            done = max(first, S - V)
            if done < last:
                nc.sync.dma_start(out=out_view[:, rows, done - (S - V) : last - (S - V)], in_=running[:, rows, done:last])
